import numpy as np
import ml_dtypes


def mxq(x, axis, fmt="e4m3"):
    dtype, down = {"e4m3": (ml_dtypes.float8_e4m3fn, 7), "e5m2": (ml_dtypes.float8_e5m2, 14)}[fmt]
    v = np.moveaxis(np.asarray(x, np.float32).astype(ml_dtypes.bfloat16).astype(np.float64), axis, -1)
    blocks = v.reshape(v.shape[:-1] + (-1, 32))
    amax = np.abs(blocks).max(-1, keepdims=True)
    byte = np.maximum(np.where(amax > 0, np.frexp(amax)[1] - 1 + 127, 0) - down, 1)
    scale = np.exp2(byte - 127.0)
    codes = (blocks / scale).astype(np.float32).astype(dtype).astype(np.float64)
    return np.moveaxis((codes * scale).reshape(v.shape), -1, axis)


WIDE = False


def mx_kscale(k):
    if not WIDE:
        return np.ones(k)
    levels = np.array([10, -10, 5, -5, 0])
    if k % 512:
        return np.exp2(np.random.permutation(np.resize(levels, k // 32))).repeat(32)
    a = np.empty((k // 512, 16))
    for p in range(k // 512):
        a[p, :8] = np.random.permutation(np.resize(levels, 8))
        for g in range(8):
            far = levels[np.abs(levels - a[p, g]) >= 10]
            a[p, g + 8] = far[np.random.randint(len(far))]
    return np.exp2(a.ravel()).repeat(32)


BF16 = ml_dtypes.bfloat16


def bf(x):
    return np.asarray(x, np.float32).astype(BF16)


def f64(x):
    return np.asarray(x).astype(np.float64)


E2M1 = np.array([0.0, 0.5, 1.0, 1.5, 2.0, 3.0, 4.0, 6.0, -0.0, -0.5, -1.0, -1.5, -2.0, -3.0, -4.0, -6.0])


def pack_weight(w, fmt):
    k, n = w.shape
    w = f64(bf(w)).reshape(k // 32, 32, n)
    amax = np.abs(w).max(1)
    if fmt == "e4m3":
        byte = np.frexp(amax)[1] - 1 + 127 - 7
    else:
        mant, ex = np.frexp(amax / 6.0)
        byte = np.where(mant > 0.5, ex, ex - 1) + 127
    byte = np.clip(np.where(amax > 0, byte, 1), 1, 254)
    scaled = (w * np.exp2(127.0 - byte)[:, None, :]).reshape(k, n).astype(np.float32)
    by_word = np.ascontiguousarray(scaled.reshape(k // 512, 128, 4, n).transpose(0, 1, 3, 2))
    if fmt == "e4m3":
        words = by_word.astype(ml_dtypes.float8_e4m3fn).view(np.uint8)
    else:
        c = by_word.astype(ml_dtypes.float4_e2m1fn).view(np.uint8) & 0xF
        words = c[..., 0::2] | (c[..., 1::2] << 4)
    return np.ascontiguousarray(words), np.ascontiguousarray(byte.astype(np.uint8).reshape(k // 512, 16, n))


def unpack_weight(words, scales, fmt):
    g, p, n, _ = words.shape
    if fmt == "e4m3":
        vals = np.ascontiguousarray(words).view(ml_dtypes.float8_e4m3fn).astype(np.float64)
    else:
        nib = np.empty((g, p, n, 4), np.uint8)
        nib[..., 0::2] = words & 0xF
        nib[..., 1::2] = words >> 4
        vals = E2M1[nib]
    vals = vals * np.repeat(np.exp2(scales.astype(np.float64) - 127.0), 8, axis=1)[..., None]
    return vals.transpose(0, 1, 3, 2).reshape(g * 512, n)
def pack4(w):
    words, scales = pack_weight(w, "e2m1")
    return words.reshape(words.shape[0], 128, -1), scales


def unpack4(words, scales):
    return unpack_weight(words.reshape(words.shape[0], 128, -1, 2), scales, "e2m1")


M, A, F, J = 1024, 2048, 1024, 512
CAP = 2.0


def setup_inputs():
    s, t = mx_kscale(A), mx_kscale(F)
    lever = np.exp(0.3 * np.random.standard_normal((M, 1)))
    load = np.random.standard_normal((A, F)) / np.sqrt(A) / s[:, None]
    mix = np.random.standard_normal((F, J)) / np.sqrt(F) / t[:, None]
    cov = np.random.standard_normal((F, A)) / np.sqrt(F) / t[:, None]
    load_words, load_scales = pack4(load)
    mix_words, mix_scales = pack_weight(mix, "e4m3")
    cov_words, cov_scales = pack_weight(cov, "e4m3")
    return {"hold": bf(np.random.standard_normal((M, A)) * lever * s),
            "load_words": load_words, "load_scales": load_scales,
            "bench": bf(0.5 * np.random.standard_normal(F)),
            "vol": bf(np.exp(0.3 * np.random.standard_normal(F)) * t),
            "mix_words": mix_words, "mix_scales": mix_scales,
            "cov_words": cov_words, "cov_scales": cov_scales,
            "spec": bf(0.7 * np.exp(0.3 * np.random.standard_normal(A)) / s)}


def reference(hold, load_words, load_scales, bench, vol, mix_words, mix_scales, cov_words, cov_scales, spec):
    h = f64(hold)
    x = (mxq(h, 1, "e4m3") @ unpack4(load_words, load_scales)) - f64(bench)
    e = CAP * np.tanh(x / CAP) * f64(vol)
    eq = mxq(e, 1, "e4m3")
    z = eq @ unpack_weight(mix_words, mix_scales, "e4m3")
    r = eq @ unpack_weight(cov_words, cov_scales, "e4m3")
    y = h * f64(spec)
    sigma = np.sqrt(np.mean(z * z, axis=1, keepdims=True) + np.mean(y * y, axis=1, keepdims=True))
    return (r + y) / sigma, z / sigma

@@ -1,0 +1,387 @@
+from contextlib import ExitStack
+
+import concourse.mybir as mybir
+from concourse.masks import make_identity
+
+M, A, F, J = 1024, 2048, 1024, 512
+FLOPS = 2 * M * A * F + 2 * M * F * (A + J)
+
+F32 = mybir.dt.float32
+BF16 = mybir.dt.bfloat16
+U32 = mybir.dt.uint32
+I32 = mybir.dt.int32
+U8 = mybir.dt.uint8
+FP8X4 = mybir.dt.float8_e4m3fn_x4
+FP4X4 = mybir.dt.float4_e2m1fn_x4
+ALU = mybir.AluOpType
+ACT = mybir.ActivationFunctionType
+
+P = 128
+ROWS = 512
+KH = A // 512
+GE = F // 512
+NR = M // P
+
+
+def tile_factor_risk_apply_f7_kernel(
+    tc, hold, load_words, load_scales, bench, vol, mix_words, mix_scales, cov_words, cov_scales, spec, out_0, out_1
+):
+    nc = tc.nc
+    with ExitStack() as ctx:
+        keep = ctx.enter_context(tc.tile_pool(name="keep", bufs=1))
+        hpool = ctx.enter_context(tc.tile_pool(name="hpool", bufs=8))
+        ypool = ctx.enter_context(tc.tile_pool(name="ypool", bufs=6))
+        grp = ctx.enter_context(tc.tile_pool(name="grp", bufs=1))
+        two = ctx.enter_context(tc.tile_pool(name="two", bufs=2))
+        small = ctx.enter_context(tc.tile_pool(name="small", bufs=8))
+        psum = ctx.enter_context(tc.psum_pool(name="psum", bufs=2))
+
+        warm = keep.tile([P, 8], F32, name="warm")
+        spec_row = keep.tile([P, A], BF16, name="spec_row")
+        ones = keep.tile([P, P], BF16, name="ones")
+        ident = keep.tile([P, P], F32, name="ident")
+        mhalf = keep.tile([P, 1], F32, name="mhalf")
+        spec_bc = keep.tile([P, A], BF16, name="spec_bc")
+        bw_raw = keep.tile([P, KH, 2 * F], U8, name="bw_raw", align_bytes=64)
+        bs_raw = keep.tile([P, KH, F], U8, name="bs_raw", align_bytes=64)
+        bw = keep.tile([P, KH, GE, 4, 2 * P], U8, name="bw", align_bytes=64)
+        bs = keep.tile([P, KH, GE, 4, P], U8, name="bs", align_bytes=64)
+        lw = keep.tile([P, GE, J], U32, name="lw", align_bytes=64)
+        vw = keep.tile([P, GE, A], U32, name="vw", align_bytes=64)
+        ls = keep.tile([P, GE, J], U8, name="ls", align_bytes=64)
+        vs = keep.tile([P, GE, A], U8, name="vs", align_bytes=64)
+        bench_in = keep.tile([P, GE, 4], BF16, name="bench_in")
+        vol_in = keep.tile([P, GE, 4], BF16, name="vol_in")
+        nbench = keep.tile([P, GE * 4], F32, name="nbench")
+        vol2 = keep.tile([P, GE * 4], F32, name="vol2")
+        junk = keep.tile([P, A], BF16, name="junk")
+
+        nc.vector.memset(warm[:], 0.0)
+        nc.vector.memset(spec_row[:].bitcast(I32), 0)
+        nc.vector.memset(bs_raw[:].rearrange("p g n -> p (g n)").bitcast(I32), 0)
+        nc.vector.memset(ones[:], 1.0)
+        make_identity(nc, ident[:])
+        nc.gpsimd.memset(mhalf[:], -0.5)
+        nc.gpsimd.memset(ls[:].rearrange("p g n -> p (g n)").bitcast(I32), 0)
+        nc.gpsimd.memset(vs[:].rearrange("p g n -> p (g n)").bitcast(I32), 0)
+
+        h_tiles = [hpool.tile([P, A], BF16, name="h", align_bytes=64) for r in range(NR)]
+
+        with tc.manual_schedule():
+            def load_scale_rows(queue, dst, src):
+                for quad in range(4):
+                    queue.dma_start(
+                        out=dst[32 * quad : 32 * quad + 4, :, :].bitcast(I32),
+                        in_=src.bitcast(I32)[:, 4 * quad : 4 * quad + 4, :].rearrange("g q n -> q g n"),
+                    )
+
+            def load_b_words(e):
+                nc.sync.dma_start(
+                    out=bw_raw[:, :, 1024 * e : 1024 * (e + 1)],
+                    in_=load_words[:, :, 1024 * e : 1024 * (e + 1)].rearrange("g p b -> p g b"),
+                )
+
+            def load_h(r):
+                nc.sync.dma_start(out=h_tiles[r][:], in_=hold[P * r : P * (r + 1), :])
+
+            load_b_words(0)
+            nc.sync.dma_start(out=spec_row[0:1, :], in_=spec.rearrange("(o n) -> o n", o=1))
+            load_scale_rows(nc.sync, bs_raw, load_scales)
+            for r in range(4):
+                load_h(r)
+            nc.sync.dma_start(out=bench_in[:], in_=bench.rearrange("(e p t) -> p e t", p=P, t=4))
+            nc.sync.dma_start(out=vol_in[:], in_=vol.rearrange("(e p t) -> p e t", p=P, t=4))
+            load_b_words(1)
+            for r in range(4, 8):
+                load_h(r)
+            for e in range(GE):
+                nc.sync.dma_start(
+                    out=lw[:, e, :].bitcast(I32), in_=mix_words[e].rearrange("p n t -> p (n t)").bitcast(I32)
+                )
+            load_scale_rows(nc.sync, ls, mix_scales)
+            load_scale_rows(nc.sync, vs, cov_scales)
+            for e in range(GE):
+                nc.sync.dma_start(
+                    out=vw[:, e, :].bitcast(I32), in_=cov_words[e].rearrange("p n t -> p (n t)").bitcast(I32)
+                )
+
+            nc.scalar.activation(out=warm[:, 0:1], in_=warm[:, 1:2], func=ACT.Tanh)
+
+            def perm_words(e, t):
+                nc.vector.tensor_copy(
+                    out=bw[:, :, e, t, :].rearrange("p g (m b) -> p g m b", b=2),
+                    in_=bw_raw[:, :, 1024 * e : 1024 * (e + 1)].rearrange("p g (m t b) -> p g t m b", t=4, b=2)[
+                        :, :, t, :, :
+                    ],
+                )
+
+            def perm_scales(eng, e):
+                eng.tensor_copy(
+                    out=bs[:, :, e, :, :],
+                    in_=bs_raw[:, :, 512 * e : 512 * (e + 1)].rearrange("p g (m t) -> p g t m", t=4),
+                )
+
+            y_tiles = {}
+            sum_y = {}
+            sum_z = {}
+            inv = {}
+            z_banks = {}
+
+            def make_y(eng, r, pieces=1):
+                if r < 6:
+                    y = ypool.tile([P, A], F32, name="y")
+                    y_tiles[r] = y[:]
+                elif r == 6:
+                    y_pair = grp.tile([P, 2, A], F32, name="y_pair", tag="grouped_t", align_bytes=64)
+                    y_tiles[6] = y_pair[:, 0, :]
+                    y_tiles[7] = y_pair[:, 1, :]
+                y = y_tiles[r]
+                step = A // pieces
+                for a in range(0, A, step):
+                    eng.tensor_tensor(
+                        out=y[:, a : a + step],
+                        in0=h_tiles[r][:, a : a + step],
+                        in1=spec_bc[:, a : a + step],
+                        op=ALU.mult,
+                    )
+
+            def square_y(r):
+                s = small.tile([P, 1], F32, name="sum_y_t")
+                sum_y[r] = s
+                nc.scalar.activation(
+                    out=junk[:], in_=y_tiles[r], func=ACT.Square, scale=A**-0.5, accum_out=s[:]
+                )
+
+            grouped = {}
+            hq = {}
+
+            def open_chunk(c):
+                g_t = grp.tile([P, KH, ROWS, 4], BF16, name="grouped_t", align_bytes=64)
+                q_t = two.tile([P, KH, ROWS], U32, name="hq_t", align_bytes=64)
+                s_t = two.tile([P, KH, ROWS], U8, name="hs_t", align_bytes=64)
+                grouped[c] = g_t
+                hq[c] = (q_t, s_t)
+
+            def transposes(r, tag, engines="ss"):
+                c, j = divmod(r, 4)
+                words = h_tiles[r][:].bitcast(F32)
+                for half in range(2):
+                    bank = psum.tile([P, 2, 2, P], F32, name="xt_bank", tag=tag)
+                    for gg in range(2):
+                        g = 2 * half + gg
+                        for u in range(2):
+                            nc.tensor.transpose(
+                                bank[:, gg, u, :], words[:, 256 * g + u : 256 * (g + 1) : 2], ident[:]
+                            )
+                    copy = nc.scalar.copy if engines[half] == "s" else nc.vector.tensor_copy
+                    copy(
+                        out=grouped[c][:, 2 * half : 2 * half + 2, P * j : P * (j + 1), :].bitcast(F32),
+                        in_=bank[:].rearrange("p g u r -> p g r u"),
+                    )
+
+            def quantize_h(c, g):
+                nc.vector.quantize_mx(
+                    out=hq[c][0][:, g, :].bitcast(FP8X4),
+                    scales=hq[c][1][:, g, :],
+                    in_=grouped[c][:, g, :, :].rearrange("p r t -> p (r t)"),
+                )
+
+            eraw = {}
+            eq = {}
+
+            def stage1(c, e, t):
+                if (c, e) not in eraw:
+                    er_t = two.tile([P, 4, ROWS], F32, name="er_t")
+                    eraw[c, e] = er_t
+                bank = psum.tile([P, ROWS], F32, name="mm_bank", tag="mm", bufs=4)
+                for g in range(KH):
+                    nc.tensor.matmul_mx(
+                        out=bank[:],
+                        lhsT=bw[:, g, e, t, :].bitcast(FP4X4),
+                        lhsT_scale=bs[:, g, e, t, :],
+                        rhs=hq[c][0][:, g, :].bitcast(FP8X4),
+                        rhs_scale=hq[c][1][:, g, :],
+                        start=(g == 0),
+                        stop=(g == KH - 1),
+                    )
+                col = 4 * e + t
+                nc.scalar.activation(
+                    out=eraw[c, e][:, t, :], in_=bank[:], func=ACT.Tanh, bias=nbench[:, col : col + 1], scale=0.5
+                )
+
+            def scale_and_quantize_e(c, e):
+                if c not in eq:
+                    eq_t = two.tile([P, GE, ROWS], U32, name="eq_t", align_bytes=64)
+                    es_t = two.tile([P, GE, ROWS], U8, name="es_t", align_bytes=64)
+                    eq[c] = (eq_t, es_t)
+                eg = two.tile([P, ROWS, 4], BF16, name="eg", align_bytes=64)
+                halves = [slice(0, ROWS // 2), slice(ROWS // 2, ROWS)]
+                for cols in halves:
+                    nc.vector.tensor_tensor(
+                        out=eg[:, cols, :],
+                        in0=eraw[c, e][:, :, cols].rearrange("p t n -> p n t"),
+                        in1=vol2[:, 4 * e : 4 * e + 4].unsqueeze(1).to_broadcast([P, ROWS // 2, 4]),
+                        op=ALU.mult,
+                    )
+                for cols in halves:
+                    nc.vector.quantize_mx(
+                        out=eq[c][0][:, e, cols].bitcast(FP8X4),
+                        scales=eq[c][1][:, e, cols],
+                        in_=eg[:, cols, :].rearrange("p n t -> p (n t)"),
+                    )
+
+            def stage2_bank(bank, r, w, s, cols):
+                c, j = divmod(r, 4)
+                mine = slice(P * j, P * (j + 1))
+                for e in range(GE):
+                    nc.tensor.matmul_mx(
+                        out=bank[:],
+                        lhsT=eq[c][0][:, e, mine].bitcast(FP8X4),
+                        lhsT_scale=eq[c][1][:, e, mine],
+                        rhs=w[:, e, cols].bitcast(FP8X4),
+                        rhs_scale=s[:, e, cols],
+                        start=(e == 0),
+                        stop=(e == GE - 1),
+                    )
+
+            def stage2_z(r):
+                bank = psum.tile([P, J], F32, name="z_bank", tag="z", bufs=2)
+                z_banks[r] = bank
+                stage2_bank(bank, r, lw, ls, slice(0, J))
+                s = small.tile([P, 1], F32, name="sum_z_t")
+                nc.scalar.activation(
+                    out=junk[:, 0:J], in_=bank[:], func=ACT.Square, scale=J**-0.5, accum_out=s[:]
+                )
+                sum_z[r] = s
+
+            def inverse_sigma(r):
+                var = small.tile([P, 1], F32, name="var_t")
+                nc.gpsimd.tensor_tensor(out=var[:], in0=sum_y[r][:], in1=sum_z[r][:], op=ALU.add)
+                inv_t = small.tile([P, 1], F32, name="inv_t")
+                nc.gpsimd.tensor_tensor(out=inv_t[:], in0=var[:], in1=mhalf[:], op=ALU.pow)
+                inv[r] = inv_t
+
+            def stage2_r(r, q):
+                cols = slice(512 * q, 512 * (q + 1))
+                bank = psum.tile([P, 512], F32, name="mm_bank", tag="mm", bufs=4)
+                stage2_bank(bank, r, vw, vs, cols)
+                y = y_tiles[r]
+                nc.vector.tensor_tensor(out=y[:, cols], in0=bank[:], in1=y[:, cols], op=ALU.add)
+
+            def finish_z(r):
+                inverse_sigma(r)
+                zo = two.tile([P, J], F32, name="zo")
+                nc.scalar.activation(out=zo[:], in_=z_banks[r][:], func=ACT.Copy, scale=inv[r][:])
+                nc.sync.dma_start(out=out_1[P * r : P * (r + 1), :], in_=zo[:])
+
+            def finish_r(eng, r, q):
+                y = y_tiles[r]
+                cols = slice(512 * q, 512 * (q + 1))
+                if eng == "s":
+                    nc.scalar.activation(out=y[:, cols], in_=y[:, cols], func=ACT.Copy, scale=inv[r][:])
+                elif eng == "g":
+                    nc.gpsimd.tensor_scalar(
+                        out=y[:, cols], in0=y[:, cols], scalar1=inv[r][:], scalar2=0.0, op0=ALU.mult, op1=ALU.add
+                    )
+                else:
+                    nc.vector.tensor_scalar(
+                        out=y[:, cols], in0=y[:, cols], scalar1=inv[r][:], scalar2=None, op0=ALU.mult
+                    )
+
+            def store_r(r, half):
+                cols = slice(1024 * half, 1024 * (half + 1))
+                nc.sync.dma_start(out=out_0[P * r : P * (r + 1), cols], in_=y_tiles[r][:, cols])
+
+            for q in range(4):
+                cols = slice(512 * q, 512 * (q + 1))
+                bank = psum.tile([P, 512], F32, name="mm_bank", tag="mm", bufs=4)
+                nc.tensor.matmul(bank[:], ones[:], spec_row[:, cols], start=True, stop=True)
+                nc.scalar.copy(out=spec_bc[:, cols], in_=bank[:])
+            for t in range(4):
+                perm_words(0, t)
+            perm_scales(nc.vector, 0)
+            open_chunk(0)
+            for r in range(4):
+                transposes(r, "xt" if r % 2 == 0 else "z")
+            make_y(nc.vector, 0)
+            perm_words(1, 0)
+            perm_words(1, 1)
+            for g in range(KH):
+                quantize_h(0, g)
+            square_y(0)
+            nc.vector.tensor_scalar(
+                out=nbench[:], in0=bench_in[:].rearrange("p e t -> p (e t)"), scalar1=-0.5, scalar2=None, op0=ALU.mult
+            )
+            nc.vector.tensor_scalar(
+                out=vol2[:], in0=vol_in[:].rearrange("p e t -> p (e t)"), scalar1=2.0, scalar2=None, op0=ALU.mult
+            )
+
+            stage1(0, 0, 0)
+            perm_words(1, 2)
+            perm_words(1, 3)
+            perm_scales(nc.vector, 1)
+            open_chunk(1)
+            stage1(0, 0, 1)
+            transposes(4, "xt")
+            make_y(nc.vector, 1)
+            stage1(0, 0, 2)
+            transposes(5, "xt")
+            make_y(nc.vector, 2)
+            stage1(0, 0, 3)
+            transposes(6, "xt")
+            scale_and_quantize_e(0, 0)
+            stage1(0, 1, 0)
+            transposes(7, "xt")
+            for g in range(KH):
+                quantize_h(1, g)
+            stage1(0, 1, 1)
+            square_y(1)
+            stage1(0, 1, 2)
+            stage1(0, 1, 3)
+
+            def tile_out(r, d="ssgg"):
+                for q in range(4):
+                    finish_r(d[q], r, q)
+                store_r(r, 0)
+                store_r(r, 1)
+
+            def stage2(r):
+                for q in range(4):
+                    stage2_r(r, q)
+
+            make_y(nc.vector, 3)
+            scale_and_quantize_e(0, 1)
+            for t in range(3):
+                stage1(1, 0, t)
+            square_y(2)
+            stage2_z(0)
+            stage2(0)
+            stage1(1, 0, 3)
+            stage1(1, 1, 0)
+            finish_z(0)
+            scale_and_quantize_e(1, 0)
+            tile_out(0)
+            stage2_z(1)
+            stage2(1)
+            for t in range(1, 4):
+                stage1(1, 1, t)
+            finish_z(1)
+            make_y(nc.vector, 4)
+            tile_out(1)
+            square_y(3)
+            stage2_z(2)
+            scale_and_quantize_e(1, 1)
+            stage2_z(3)
+            finish_z(2)
+            stage2(2)
+            for r in range(3, NR):
+                if r + 1 < NR:
+                    stage2_z(r + 1)
+                stage2(r)
+                if r + 2 < NR:
+                    make_y(nc.vector, r + 2)
+                finish_z(r)
+                tile_out(r - 1)
+                if r + 1 < NR:
+                    square_y(r + 1)
+            tile_out(NR - 1, "sgvv")

@@ -42,10 +42,10 @@ def tile_factor_risk_apply_f7_kernel(
         ident = keep.tile([P, P], F32, name="ident")
         mhalf = keep.tile([P, 1], F32, name="mhalf")
         spec_bc = keep.tile([P, A], BF16, name="spec_bc")
-        bw_raw = keep.tile([P, KH, 2 * F], U8, name="bw_raw", align_bytes=64)
+        bw_raw = [keep.tile([P, KH, F], U8, name="bw_raw%d" % e, align_bytes=64) for e in range(GE)]
         bs_raw = keep.tile([P, KH, F], U8, name="bs_raw", align_bytes=64)
-        bw = keep.tile([P, KH, GE, 4, 2 * P], U8, name="bw", align_bytes=64)
-        bs = keep.tile([P, KH, GE, 4, P], U8, name="bs", align_bytes=64)
+        bw = [keep.tile([P, 4, KH, 2 * P], U8, name="bw%d" % e, align_bytes=64) for e in range(GE)]
+        bs = keep.tile([P, 4, KH, GE, P], U8, name="bs", align_bytes=64)
         lw = keep.tile([P, GE, J], U32, name="lw", align_bytes=64)
         vw = keep.tile([P, GE, A], U32, name="vw", align_bytes=64)
         ls = keep.tile([P, GE, J], U8, name="ls", align_bytes=64)
@@ -56,9 +56,9 @@ def tile_factor_risk_apply_f7_kernel(
         vol2 = keep.tile([P, GE * 4], F32, name="vol2")
         junk = keep.tile([P, A], BF16, name="junk")
 
-        nc.vector.memset(warm[:], 0.0)
-        nc.vector.memset(spec_row[:].bitcast(I32), 0)
         nc.vector.memset(bs_raw[:].rearrange("p g n -> p (g n)").bitcast(I32), 0)
+        nc.vector.memset(spec_row[:].bitcast(I32), 0)
+        nc.vector.memset(warm[:], 0.0)
         nc.vector.memset(ones[:], 1.0)
         make_identity(nc, ident[:])
         nc.gpsimd.memset(mhalf[:], -0.5)
@@ -77,16 +77,16 @@ def tile_factor_risk_apply_f7_kernel(
 
             def load_b_words(e):
                 nc.sync.dma_start(
-                    out=bw_raw[:, :, 1024 * e : 1024 * (e + 1)],
+                    out=bw_raw[e][:],
                     in_=load_words[:, :, 1024 * e : 1024 * (e + 1)].rearrange("g p b -> p g b"),
                 )
 
             def load_h(r):
                 nc.sync.dma_start(out=h_tiles[r][:], in_=hold[P * r : P * (r + 1), :])
 
-            load_b_words(0)
-            nc.sync.dma_start(out=spec_row[0:1, :], in_=spec.rearrange("(o n) -> o n", o=1))
             load_scale_rows(nc.sync, bs_raw, load_scales)
+            nc.sync.dma_start(out=spec_row[0:1, :], in_=spec.rearrange("(o n) -> o n", o=1))
+            load_b_words(0)
             for r in range(4):
                 load_h(r)
             nc.sync.dma_start(out=bench_in[:], in_=bench.rearrange("(e p t) -> p e t", p=P, t=4))
@@ -107,18 +107,16 @@ def tile_factor_risk_apply_f7_kernel(
 
             nc.scalar.activation(out=warm[:, 0:1], in_=warm[:, 1:2], func=ACT.Tanh)
 
-            def perm_words(e, t):
+            def perm_words(e):
                 nc.vector.tensor_copy(
-                    out=bw[:, :, e, t, :].rearrange("p g (m b) -> p g m b", b=2),
-                    in_=bw_raw[:, :, 1024 * e : 1024 * (e + 1)].rearrange("p g (m t b) -> p g t m b", t=4, b=2)[
-                        :, :, t, :, :
-                    ],
+                    out=bw[e][:].rearrange("p t g (m b) -> p t (g m) b", b=2),
+                    in_=bw_raw[e][:].rearrange("p g (m t b) -> p t (g m) b", t=4, b=2),
                 )
 
-            def perm_scales(eng, e):
-                eng.tensor_copy(
-                    out=bs[:, :, e, :, :],
-                    in_=bs_raw[:, :, 512 * e : 512 * (e + 1)].rearrange("p g (m t) -> p g t m", t=4),
+            def perm_scales():
+                nc.vector.tensor_copy(
+                    out=bs[:].rearrange("p t g e m -> p t (g e m)"),
+                    in_=bs_raw[:].rearrange("p g (e m t) -> p t (g e m)", e=GE, t=4),
                 )
 
             y_tiles = {}
@@ -127,17 +125,17 @@ def tile_factor_risk_apply_f7_kernel(
             inv = {}
             z_banks = {}
 
-            def make_y(eng, r, pieces=1):
+            def make_y(eng, r, pieces=1, todo=None):
                 if r < 6:
                     y = ypool.tile([P, A], F32, name="y")
                     y_tiles[r] = y[:]
-                elif r == 6:
+                elif r == 6 and not y_tiles.get(6):
                     y_pair = grp.tile([P, 2, A], F32, name="y_pair", tag="grouped_t", align_bytes=64)
                     y_tiles[6] = y_pair[:, 0, :]
                     y_tiles[7] = y_pair[:, 1, :]
                 y = y_tiles[r]
                 step = A // pieces
-                for a in range(0, A, step):
+                for a in range(0, A, step) if todo is None else [step * i for i in todo]:
                     eng.tensor_tensor(
                         out=y[:, a : a + step],
                         in0=h_tiles[r][:, a : a + step],
@@ -197,8 +195,8 @@ def tile_factor_risk_apply_f7_kernel(
                 for g in range(KH):
                     nc.tensor.matmul_mx(
                         out=bank[:],
-                        lhsT=bw[:, g, e, t, :].bitcast(FP4X4),
-                        lhsT_scale=bs[:, g, e, t, :],
+                        lhsT=bw[e][:, t, g, :].bitcast(FP4X4),
+                        lhsT_scale=bs[:, t, g, e, :],
                         rhs=hq[c][0][:, g, :].bitcast(FP8X4),
                         rhs_scale=hq[c][1][:, g, :],
                         start=(g == 0),
@@ -209,26 +207,31 @@ def tile_factor_risk_apply_f7_kernel(
                     out=eraw[c, e][:, t, :], in_=bank[:], func=ACT.Tanh, bias=nbench[:, col : col + 1], scale=0.5
                 )
 
-            def scale_and_quantize_e(c, e):
+            eg = {}
+
+            def scale_e(c, e, half):
+                if (c, e) not in eg:
+                    eg_t = two.tile([P, ROWS, 4], BF16, name="eg_t", align_bytes=64)
+                    eg[c, e] = eg_t
+                cols = slice(256 * half, 256 * (half + 1))
+                nc.vector.tensor_tensor(
+                    out=eg[c, e][:, cols, :],
+                    in0=eraw[c, e][:, :, cols].rearrange("p t n -> p n t"),
+                    in1=vol2[:, 4 * e : 4 * e + 4].unsqueeze(1).to_broadcast([P, 256, 4]),
+                    op=ALU.mult,
+                )
+
+            def quantize_e(c, e, half):
                 if c not in eq:
                     eq_t = two.tile([P, GE, ROWS], U32, name="eq_t", align_bytes=64)
                     es_t = two.tile([P, GE, ROWS], U8, name="es_t", align_bytes=64)
                     eq[c] = (eq_t, es_t)
-                eg = two.tile([P, ROWS, 4], BF16, name="eg", align_bytes=64)
-                halves = [slice(0, ROWS // 2), slice(ROWS // 2, ROWS)]
-                for cols in halves:
-                    nc.vector.tensor_tensor(
-                        out=eg[:, cols, :],
-                        in0=eraw[c, e][:, :, cols].rearrange("p t n -> p n t"),
-                        in1=vol2[:, 4 * e : 4 * e + 4].unsqueeze(1).to_broadcast([P, ROWS // 2, 4]),
-                        op=ALU.mult,
-                    )
-                for cols in halves:
-                    nc.vector.quantize_mx(
-                        out=eq[c][0][:, e, cols].bitcast(FP8X4),
-                        scales=eq[c][1][:, e, cols],
-                        in_=eg[:, cols, :].rearrange("p n t -> p (n t)"),
-                    )
+                cols = slice(256 * half, 256 * (half + 1)) if half is not None else slice(0, ROWS)
+                nc.vector.quantize_mx(
+                    out=eq[c][0][:, e, cols].bitcast(FP8X4),
+                    scales=eq[c][1][:, e, cols],
+                    in_=eg[c, e][:, cols, :].rearrange("p n t -> p (n t)"),
+                )
 
             def stage2_bank(bank, r, w, s, cols):
                 c, j = divmod(r, 4)
@@ -249,10 +252,12 @@ def tile_factor_risk_apply_f7_kernel(
                 z_banks[r] = bank
                 stage2_bank(bank, r, lw, ls, slice(0, J))
                 s = small.tile([P, 1], F32, name="sum_z_t")
-                nc.scalar.activation(
-                    out=junk[:, 0:J], in_=bank[:], func=ACT.Square, scale=J**-0.5, accum_out=s[:]
-                )
                 sum_z[r] = s
+
+            def square_z(r):
+                nc.scalar.activation(
+                    out=junk[:, 0:J], in_=z_banks[r][:], func=ACT.Square, scale=J**-0.5, accum_out=sum_z[r][:]
+                )
 
             def inverse_sigma(r):
                 var = small.tile([P, 1], F32, name="var_t")
@@ -292,96 +297,112 @@ def tile_factor_risk_apply_f7_kernel(
                 cols = slice(1024 * half, 1024 * (half + 1))
                 nc.sync.dma_start(out=out_0[P * r : P * (r + 1), cols], in_=y_tiles[r][:, cols])
 
-            for q in range(4):
+            def spread_spec(q):
                 cols = slice(512 * q, 512 * (q + 1))
                 bank = psum.tile([P, 512], F32, name="mm_bank", tag="mm", bufs=4)
                 nc.tensor.matmul(bank[:], ones[:], spec_row[:, cols], start=True, stop=True)
                 nc.scalar.copy(out=spec_bc[:, cols], in_=bank[:])
-            for t in range(4):
-                perm_words(0, t)
-            perm_scales(nc.vector, 0)
-            open_chunk(0)
-            for r in range(4):
-                transposes(r, "xt" if r % 2 == 0 else "z")
-            make_y(nc.vector, 0)
-            perm_words(1, 0)
-            perm_words(1, 1)
-            for g in range(KH):
-                quantize_h(0, g)
-            square_y(0)
-            nc.vector.tensor_scalar(
-                out=nbench[:], in0=bench_in[:].rearrange("p e t -> p (e t)"), scalar1=-0.5, scalar2=None, op0=ALU.mult
-            )
-            nc.vector.tensor_scalar(
-                out=vol2[:], in0=vol_in[:].rearrange("p e t -> p (e t)"), scalar1=2.0, scalar2=None, op0=ALU.mult
-            )
-
-            stage1(0, 0, 0)
-            perm_words(1, 2)
-            perm_words(1, 3)
-            perm_scales(nc.vector, 1)
-            open_chunk(1)
-            stage1(0, 0, 1)
-            transposes(4, "xt")
-            make_y(nc.vector, 1)
-            stage1(0, 0, 2)
-            transposes(5, "xt")
-            make_y(nc.vector, 2)
-            stage1(0, 0, 3)
-            transposes(6, "xt")
-            scale_and_quantize_e(0, 0)
-            stage1(0, 1, 0)
-            transposes(7, "xt")
-            for g in range(KH):
-                quantize_h(1, g)
-            stage1(0, 1, 1)
-            square_y(1)
-            stage1(0, 1, 2)
-            stage1(0, 1, 3)
-
-            def tile_out(r, d="ssgg"):
-                for q in range(4):
-                    finish_r(d[q], r, q)
-                store_r(r, 0)
-                store_r(r, 1)
 
             def stage2(r):
                 for q in range(4):
                     stage2_r(r, q)
 
+            def tile_out(r, d):
+                for q in range(4):
+                    finish_r(d[q], r, q)
+                store_r(r, 0)
+                store_r(r, 1)
+
+            for q in range(4):
+                spread_spec(q)
+            for vec, raw, factor in ((nbench, bench_in, -0.5), (vol2, vol_in, 2.0)):
+                nc.gpsimd.tensor_scalar(
+                    out=vec[:],
+                    in0=raw[:].rearrange("p e t -> p (e t)"),
+                    scalar1=factor,
+                    scalar2=0.0,
+                    op0=ALU.mult,
+                    op1=ALU.add,
+                )
+            perm_scales()
+            perm_words(0)
+            open_chunk(0)
+            for r in range(4):
+                transposes(r, "xt" if r % 2 == 0 else "z")
+            make_y(nc.vector, 0)
+            for g in range(KH):
+                quantize_h(0, g)
+            square_y(0)
+            make_y(nc.vector, 1)
+
+            open_chunk(1)
+            stage1(0, 0, 0)
+            perm_words(1)
+            stage1(0, 0, 1)
+            transposes(4, "xt")
+            make_y(nc.vector, 2)
+            stage1(0, 0, 2)
+            transposes(5, "xt")
+            stage1(0, 0, 3)
+            transposes(6, "xt")
+            scale_e(0, 0, 0)
+            scale_e(0, 0, 1)
+            stage1(0, 1, 0)
+            transposes(7, "xt")
+            square_y(1)
+            quantize_e(0, 0, None)
+            for g in range(KH):
+                quantize_h(1, g)
+            for t in range(1, 4):
+                stage1(0, 1, t)
             make_y(nc.vector, 3)
-            scale_and_quantize_e(0, 1)
+            for half in range(2):
+                scale_e(0, 1, half)
+            for half in range(2):
+                quantize_e(0, 1, half)
+            square_y(2)
+
             for t in range(3):
                 stage1(1, 0, t)
-            square_y(2)
+            make_y(nc.vector, 4)
             stage2_z(0)
+            square_z(0)
             stage2(0)
             stage1(1, 0, 3)
             stage1(1, 1, 0)
             finish_z(0)
-            scale_and_quantize_e(1, 0)
-            tile_out(0)
+            scale_e(1, 0, 0)
+            scale_e(1, 0, 1)
+            square_y(3)
+            tile_out(0, "ssgg")
             stage2_z(1)
+            square_z(1)
             stage2(1)
+            quantize_e(1, 0, None)
             for t in range(1, 4):
                 stage1(1, 1, t)
             finish_z(1)
-            make_y(nc.vector, 4)
-            tile_out(1)
-            square_y(3)
+            make_y(nc.vector, 5)
+            tile_out(1, "ssgg")
             stage2_z(2)
-            scale_and_quantize_e(1, 1)
-            stage2_z(3)
+            for half in range(2):
+                scale_e(1, 1, half)
+            for half in range(2):
+                quantize_e(1, 1, half)
+            square_z(2)
             finish_z(2)
+            stage2_z(3)
             stage2(2)
+            square_z(3)
             for r in range(3, NR):
                 if r + 1 < NR:
                     stage2_z(r + 1)
+                    square_z(r + 1)
                 stage2(r)
-                if r + 2 < NR:
+                if r in (4, 5):
                     make_y(nc.vector, r + 2)
                 finish_z(r)
-                tile_out(r - 1)
-                if r + 1 < NR:
+                tile_out(r - 1, "gggg" if r == 6 else "sggg")
+                if r + 1 < NR :
                     square_y(r + 1)
             tile_out(NR - 1, "sgvv")

@@ -215,9 +215,9 @@ def tile_factor_risk_apply_f7_kernel(
                     eg[c, e] = eg_t
                 cols = slice(256 * half, 256 * (half + 1))
                 nc.vector.tensor_tensor(
-                    out=eg[c, e][:, cols, :],
-                    in0=eraw[c, e][:, :, cols].rearrange("p t n -> p n t"),
-                    in1=vol2[:, 4 * e : 4 * e + 4].unsqueeze(1).to_broadcast([P, 256, 4]),
+                    out=eg[c, e][:, cols, :].rearrange("p (n i) t -> p n t i", i=4),
+                    in0=eraw[c, e][:, :, cols].rearrange("p t (n i) -> p n t i", i=4),
+                    in1=vol2[:, 4 * e : 4 * e + 4].unsqueeze(1).unsqueeze(3).to_broadcast([P, 64, 4, 4]),
                     op=ALU.mult,
                 )
 
@@ -374,7 +374,7 @@ def tile_factor_risk_apply_f7_kernel(
             scale_e(1, 0, 0)
             scale_e(1, 0, 1)
             square_y(3)
-            tile_out(0, "ssgg")
+            tile_out(0, "ssss")
             stage2_z(1)
             square_z(1)
             stage2(1)
@@ -383,7 +383,7 @@ def tile_factor_risk_apply_f7_kernel(
                 stage1(1, 1, t)
             finish_z(1)
             make_y(nc.vector, 5)
-            tile_out(1, "ssgg")
+            tile_out(1, "ssss")
             stage2_z(2)
             for half in range(2):
                 scale_e(1, 1, half)

@@ -17,10 +17,11 @@ ALU = mybir.AluOpType
 ACT = mybir.ActivationFunctionType
 
 P = 128
-ROWS = 512
+PACK = 4
 KH = A // 512
 GE = F // 512
 NR = M // P
+BANK = 512
 
 
 def tile_factor_risk_apply_f7_kernel(
@@ -31,8 +32,7 @@ def tile_factor_risk_apply_f7_kernel(
         keep = ctx.enter_context(tc.tile_pool(name="keep", bufs=1))
         hpool = ctx.enter_context(tc.tile_pool(name="hpool", bufs=8))
         ypool = ctx.enter_context(tc.tile_pool(name="ypool", bufs=6))
-        grp = ctx.enter_context(tc.tile_pool(name="grp", bufs=1))
-        two = ctx.enter_context(tc.tile_pool(name="two", bufs=2))
+        work = ctx.enter_context(tc.tile_pool(name="work", bufs=3))
         small = ctx.enter_context(tc.tile_pool(name="small", bufs=8))
         psum = ctx.enter_context(tc.psum_pool(name="psum", bufs=2))
 
@@ -44,22 +44,22 @@ def tile_factor_risk_apply_f7_kernel(
         spec_bc = keep.tile([P, A], BF16, name="spec_bc")
         bw_raw = [keep.tile([P, KH, F], U8, name="bw_raw%d" % e, align_bytes=64) for e in range(GE)]
         bs_raw = keep.tile([P, KH, F], U8, name="bs_raw", align_bytes=64)
-        bw = [keep.tile([P, 4, KH, 2 * P], U8, name="bw%d" % e, align_bytes=64) for e in range(GE)]
-        bs = keep.tile([P, 4, KH, GE, P], U8, name="bs", align_bytes=64)
+        bw = [keep.tile([P, PACK, KH, 2 * P], U8, name="bw%d" % e, align_bytes=64) for e in range(GE)]
+        bs = [keep.tile([P, PACK, KH, P], U8, name="bs%d" % e, align_bytes=64) for e in range(GE)]
         lw = keep.tile([P, GE, J], U32, name="lw", align_bytes=64)
         vw = keep.tile([P, GE, A], U32, name="vw", align_bytes=64)
         ls = keep.tile([P, GE, J], U8, name="ls", align_bytes=64)
         vs = keep.tile([P, GE, A], U8, name="vs", align_bytes=64)
-        bench_in = keep.tile([P, GE, 4], BF16, name="bench_in")
-        vol_in = keep.tile([P, GE, 4], BF16, name="vol_in")
-        nbench = keep.tile([P, GE * 4], F32, name="nbench")
-        vol2 = keep.tile([P, GE * 4], F32, name="vol2")
+        bench_in = keep.tile([P, GE, PACK], BF16, name="bench_in")
+        vol_in = keep.tile([P, GE, PACK], BF16, name="vol_in")
+        nbench = keep.tile([P, GE, PACK], F32, name="nbench")
+        vol2 = keep.tile([P, GE, P // PACK, PACK], F32, name="vol2")
         junk = keep.tile([P, A], BF16, name="junk")
 
         nc.vector.memset(bs_raw[:].rearrange("p g n -> p (g n)").bitcast(I32), 0)
+        nc.vector.memset(ones[:], 1.0)
         nc.vector.memset(spec_row[:].bitcast(I32), 0)
         nc.vector.memset(warm[:], 0.0)
-        nc.vector.memset(ones[:], 1.0)
         make_identity(nc, ident[:])
         nc.gpsimd.memset(mhalf[:], -0.5)
         nc.gpsimd.memset(ls[:].rearrange("p g n -> p (g n)").bitcast(I32), 0)
@@ -68,179 +68,149 @@ def tile_factor_risk_apply_f7_kernel(
         h_tiles = [hpool.tile([P, A], BF16, name="h", align_bytes=64) for r in range(NR)]
 
         with tc.manual_schedule():
-            def load_scale_rows(queue, dst, src):
+            def load_scale_rows(dst, src):
                 for quad in range(4):
-                    queue.dma_start(
+                    nc.sync.dma_start(
                         out=dst[32 * quad : 32 * quad + 4, :, :].bitcast(I32),
                         in_=src.bitcast(I32)[:, 4 * quad : 4 * quad + 4, :].rearrange("g q n -> q g n"),
                     )
 
             def load_b_words(e):
                 nc.sync.dma_start(
-                    out=bw_raw[e][:],
-                    in_=load_words[:, :, 1024 * e : 1024 * (e + 1)].rearrange("g p b -> p g b"),
+                    out=bw_raw[e][:], in_=load_words[:, :, F * e : F * (e + 1)].rearrange("g p b -> p g b")
                 )
 
             def load_h(r):
                 nc.sync.dma_start(out=h_tiles[r][:], in_=hold[P * r : P * (r + 1), :])
 
-            load_scale_rows(nc.sync, bs_raw, load_scales)
-            nc.sync.dma_start(out=spec_row[0:1, :], in_=spec.rearrange("(o n) -> o n", o=1))
+            def load_words_of(dst, src, e):
+                nc.sync.dma_start(out=dst[:, e, :].bitcast(I32), in_=src[e].rearrange("p n t -> p (n t)").bitcast(I32))
+
+            load_scale_rows(bs_raw, load_scales)
             load_b_words(0)
-            for r in range(4):
-                load_h(r)
-            nc.sync.dma_start(out=bench_in[:], in_=bench.rearrange("(e p t) -> p e t", p=P, t=4))
-            nc.sync.dma_start(out=vol_in[:], in_=vol.rearrange("(e p t) -> p e t", p=P, t=4))
+            nc.sync.dma_start(out=spec_row[0:1, :], in_=spec.rearrange("(o n) -> o n", o=1))
+            load_h(0)
             load_b_words(1)
-            for r in range(4, 8):
+            load_h(1)
+            nc.sync.dma_start(out=bench_in[:], in_=bench.rearrange("(e p t) -> p e t", p=P, t=PACK))
+            nc.sync.dma_start(out=vol_in[:], in_=vol.rearrange("(e p t) -> p e t", p=P, t=PACK))
+            load_h(2)
+            load_scale_rows(ls, mix_scales)
+            load_scale_rows(vs, cov_scales)
+            for e in range(GE):
+                load_words_of(lw, mix_words, e)
+            for e in range(GE):
+                load_words_of(vw, cov_words, e)
+            for r in range(3, NR):
                 load_h(r)
-            for e in range(GE):
-                nc.sync.dma_start(
-                    out=lw[:, e, :].bitcast(I32), in_=mix_words[e].rearrange("p n t -> p (n t)").bitcast(I32)
-                )
-            load_scale_rows(nc.sync, ls, mix_scales)
-            load_scale_rows(nc.sync, vs, cov_scales)
-            for e in range(GE):
-                nc.sync.dma_start(
-                    out=vw[:, e, :].bitcast(I32), in_=cov_words[e].rearrange("p n t -> p (n t)").bitcast(I32)
-                )
 
             nc.scalar.activation(out=warm[:, 0:1], in_=warm[:, 1:2], func=ACT.Tanh)
 
-            def perm_words(e):
+            def permute_words(e):
                 nc.vector.tensor_copy(
                     out=bw[e][:].rearrange("p t g (m b) -> p t (g m) b", b=2),
-                    in_=bw_raw[e][:].rearrange("p g (m t b) -> p t (g m) b", t=4, b=2),
+                    in_=bw_raw[e][:].rearrange("p g (m t b) -> p t (g m) b", t=PACK, b=2),
                 )
 
-            def perm_scales():
+            def permute_scales(e):
                 nc.vector.tensor_copy(
-                    out=bs[:].rearrange("p t g e m -> p t (g e m)"),
-                    in_=bs_raw[:].rearrange("p g (e m t) -> p t (g e m)", e=GE, t=4),
+                    out=bs[e][:].rearrange("p t g m -> p g t m"),
+                    in_=bs_raw[:, :, BANK * e : BANK * (e + 1)].rearrange("p g (m t) -> p g t m", t=PACK),
                 )
 
-            y_tiles = {}
-            sum_y = {}
-            sum_z = {}
-            inv = {}
-            z_banks = {}
+            grouped, h_codes, x_raw, e_grouped, e_codes = {}, {}, {}, {}, {}
+            y_tiles, sums, inv, z_banks = {}, {}, {}, {}
 
-            def make_y(eng, r, pieces=1, todo=None):
-                if r < 6:
-                    y = ypool.tile([P, A], F32, name="y")
-                    y_tiles[r] = y[:]
-                elif r == 6 and not y_tiles.get(6):
-                    y_pair = grp.tile([P, 2, A], F32, name="y_pair", tag="grouped_t", align_bytes=64)
-                    y_tiles[6] = y_pair[:, 0, :]
-                    y_tiles[7] = y_pair[:, 1, :]
-                y = y_tiles[r]
-                step = A // pieces
-                for a in range(0, A, step) if todo is None else [step * i for i in todo]:
-                    eng.tensor_tensor(
-                        out=y[:, a : a + step],
-                        in0=h_tiles[r][:, a : a + step],
-                        in1=spec_bc[:, a : a + step],
-                        op=ALU.mult,
-                    )
-
-            def square_y(r):
-                s = small.tile([P, 1], F32, name="sum_y_t")
-                sum_y[r] = s
-                nc.scalar.activation(
-                    out=junk[:], in_=y_tiles[r], func=ACT.Square, scale=A**-0.5, accum_out=s[:]
-                )
-
-            grouped = {}
-            hq = {}
-
-            def open_chunk(c):
-                g_t = grp.tile([P, KH, ROWS, 4], BF16, name="grouped_t", align_bytes=64)
-                q_t = two.tile([P, KH, ROWS], U32, name="hq_t", align_bytes=64)
-                s_t = two.tile([P, KH, ROWS], U8, name="hs_t", align_bytes=64)
-                grouped[c] = g_t
-                hq[c] = (q_t, s_t)
-
-            def transposes(r, tag, engines="ss"):
-                c, j = divmod(r, 4)
+            def transpose_h(r):
                 words = h_tiles[r][:].bitcast(F32)
+                grp = work.tile([P, KH, P, PACK], BF16, name="grp", align_bytes=64)
+                grouped[r] = grp
                 for half in range(2):
-                    bank = psum.tile([P, 2, 2, P], F32, name="xt_bank", tag=tag)
+                    bank = psum.tile([P, 2, 2, P], F32, name="xt_bank", tag="xt", bufs=2)
                     for gg in range(2):
                         g = 2 * half + gg
                         for u in range(2):
                             nc.tensor.transpose(
                                 bank[:, gg, u, :], words[:, 256 * g + u : 256 * (g + 1) : 2], ident[:]
                             )
-                    copy = nc.scalar.copy if engines[half] == "s" else nc.vector.tensor_copy
-                    copy(
-                        out=grouped[c][:, 2 * half : 2 * half + 2, P * j : P * (j + 1), :].bitcast(F32),
+                    nc.scalar.copy(
+                        out=grp[:, 2 * half : 2 * half + 2, :, :].bitcast(F32),
                         in_=bank[:].rearrange("p g u r -> p g r u"),
                     )
 
-            def quantize_h(c, g):
+            def quantize_h(r):
+                hq = work.tile([P, KH, P], U32, name="hq", align_bytes=64)
+                hs = work.tile([P, KH, P], U8, name="hs", align_bytes=64)
+                h_codes[r] = (hq, hs)
                 nc.vector.quantize_mx(
-                    out=hq[c][0][:, g, :].bitcast(FP8X4),
-                    scales=hq[c][1][:, g, :],
-                    in_=grouped[c][:, g, :, :].rearrange("p r t -> p (r t)"),
+                    out=hq[:].rearrange("p g r -> p (g r)").bitcast(FP8X4),
+                    scales=hs[:].rearrange("p g r -> p (g r)"),
+                    in_=grouped[r][:].rearrange("p g r t -> p (g r t)"),
                 )
 
-            eraw = {}
-            eq = {}
+            def make_y(r):
+                y = ypool.tile([P, A], F32, name="y")
+                y_tiles[r] = y
+                nc.vector.tensor_tensor(out=y[:], in0=h_tiles[r][:], in1=spec_bc[:], op=ALU.mult)
 
-            def stage1(c, e, t):
-                if (c, e) not in eraw:
-                    er_t = two.tile([P, 4, ROWS], F32, name="er_t")
-                    eraw[c, e] = er_t
-                bank = psum.tile([P, ROWS], F32, name="mm_bank", tag="mm", bufs=4)
-                for g in range(KH):
-                    nc.tensor.matmul_mx(
-                        out=bank[:],
-                        lhsT=bw[e][:, t, g, :].bitcast(FP4X4),
-                        lhsT_scale=bs[:, t, g, e, :],
-                        rhs=hq[c][0][:, g, :].bitcast(FP8X4),
-                        rhs_scale=hq[c][1][:, g, :],
-                        start=(g == 0),
-                        stop=(g == KH - 1),
-                    )
-                col = 4 * e + t
-                nc.scalar.activation(
-                    out=eraw[c, e][:, t, :], in_=bank[:], func=ACT.Tanh, bias=nbench[:, col : col + 1], scale=0.5
-                )
+            def square_y(r):
+                s = small.tile([P, 1], F32, name="sum_y")
+                sums[r] = [s]
+                nc.scalar.activation(out=junk[:], in_=y_tiles[r][:], func=ACT.Square, scale=A**-0.5, accum_out=s[:])
 
-            eg = {}
+            def stage1(r):
+                xr = work.tile([P, PACK, GE, P], F32, name="xr")
+                x_raw[r] = xr
+                hq, hs = h_codes[r]
+                for e in range(GE):
+                    bank = psum.tile([P, PACK, P], F32, name="x_bank", tag="x", bufs=2)
+                    for t in range(PACK):
+                        for g in range(KH):
+                            nc.tensor.matmul_mx(
+                                out=bank[:, t, :],
+                                lhsT=bw[e][:, t, g, :].bitcast(FP4X4),
+                                lhsT_scale=bs[e][:, t, g, :],
+                                rhs=hq[:, g, :].bitcast(FP8X4),
+                                rhs_scale=hs[:, g, :],
+                                start=(g == 0),
+                                stop=(g == KH - 1),
+                            )
+                    for t in range(PACK):
+                        nc.scalar.activation(
+                            out=xr[:, t, e, :],
+                            in_=bank[:, t, :],
+                            func=ACT.Tanh,
+                            bias=nbench[:, e, t : t + 1],
+                            scale=0.5,
+                        )
 
-            def scale_e(c, e, half):
-                if (c, e) not in eg:
-                    eg_t = two.tile([P, ROWS, 4], BF16, name="eg_t", align_bytes=64)
-                    eg[c, e] = eg_t
-                cols = slice(256 * half, 256 * (half + 1))
+            def scale_e(r):
+                eg = work.tile([P, GE, P, PACK], BF16, name="eg", align_bytes=64)
+                e_grouped[r] = eg
                 nc.vector.tensor_tensor(
-                    out=eg[c, e][:, cols, :].rearrange("p (n i) t -> p n t i", i=4),
-                    in0=eraw[c, e][:, :, cols].rearrange("p t (n i) -> p n t i", i=4),
-                    in1=vol2[:, 4 * e : 4 * e + 4].unsqueeze(1).unsqueeze(3).to_broadcast([P, 64, 4, 4]),
+                    out=eg[:].rearrange("p e (n i) t -> p (e n) t i", i=4),
+                    in0=x_raw[r][:].rearrange("p t e (n i) -> p (e n) t i", i=4),
+                    in1=vol2[:].rearrange("p e n t -> p (e n) t").unsqueeze(3).to_broadcast([P, GE * P // 4, PACK, 4]),
                     op=ALU.mult,
                 )
 
-            def quantize_e(c, e, half):
-                if c not in eq:
-                    eq_t = two.tile([P, GE, ROWS], U32, name="eq_t", align_bytes=64)
-                    es_t = two.tile([P, GE, ROWS], U8, name="es_t", align_bytes=64)
-                    eq[c] = (eq_t, es_t)
-                cols = slice(256 * half, 256 * (half + 1)) if half is not None else slice(0, ROWS)
+            def quantize_e(r):
+                eq = work.tile([P, GE, P], U32, name="eq", align_bytes=64)
+                es = work.tile([P, GE, P], U8, name="es", align_bytes=64)
+                e_codes[r] = (eq, es)
                 nc.vector.quantize_mx(
-                    out=eq[c][0][:, e, cols].bitcast(FP8X4),
-                    scales=eq[c][1][:, e, cols],
-                    in_=eg[c, e][:, cols, :].rearrange("p n t -> p (n t)"),
+                    out=eq[:].rearrange("p e n -> p (e n)").bitcast(FP8X4),
+                    scales=es[:].rearrange("p e n -> p (e n)"),
+                    in_=e_grouped[r][:].rearrange("p e n t -> p (e n t)"),
                 )
 
             def stage2_bank(bank, r, w, s, cols):
-                c, j = divmod(r, 4)
-                mine = slice(P * j, P * (j + 1))
+                eq, es = e_codes[r]
                 for e in range(GE):
                     nc.tensor.matmul_mx(
                         out=bank[:],
-                        lhsT=eq[c][0][:, e, mine].bitcast(FP8X4),
-                        lhsT_scale=eq[c][1][:, e, mine],
+                        lhsT=eq[:, e, :].bitcast(FP8X4),
+                        lhsT_scale=es[:, e, :],
                         rhs=w[:, e, cols].bitcast(FP8X4),
                         rhs_scale=s[:, e, cols],
                         start=(e == 0),
@@ -248,161 +218,94 @@ def tile_factor_risk_apply_f7_kernel(
                     )
 
             def stage2_z(r):
-                bank = psum.tile([P, J], F32, name="z_bank", tag="z", bufs=2)
+                bank = psum.tile([P, J], F32, name="z_bank", tag="z", bufs=1)
                 z_banks[r] = bank
                 stage2_bank(bank, r, lw, ls, slice(0, J))
-                s = small.tile([P, 1], F32, name="sum_z_t")
-                sum_z[r] = s
-
-            def square_z(r):
-                nc.scalar.activation(
-                    out=junk[:, 0:J], in_=z_banks[r][:], func=ACT.Square, scale=J**-0.5, accum_out=sum_z[r][:]
-                )
+                s = small.tile([P, 1], F32, name="sum_z")
+                sums[r].append(s)
+                nc.scalar.activation(out=junk[:, 0:J], in_=bank[:], func=ACT.Square, scale=J**-0.5, accum_out=s[:])
 
             def inverse_sigma(r):
-                var = small.tile([P, 1], F32, name="var_t")
-                nc.gpsimd.tensor_tensor(out=var[:], in0=sum_y[r][:], in1=sum_z[r][:], op=ALU.add)
+                var = small.tile([P, 1], F32, name="var")
+                nc.gpsimd.tensor_tensor(out=var[:], in0=sums[r][0][:], in1=sums[r][1][:], op=ALU.add)
                 inv_t = small.tile([P, 1], F32, name="inv_t")
                 nc.gpsimd.tensor_tensor(out=inv_t[:], in0=var[:], in1=mhalf[:], op=ALU.pow)
                 inv[r] = inv_t
 
-            def stage2_r(r, q):
-                cols = slice(512 * q, 512 * (q + 1))
-                bank = psum.tile([P, 512], F32, name="mm_bank", tag="mm", bufs=4)
-                stage2_bank(bank, r, vw, vs, cols)
+            def stage2_r(r, quarters):
                 y = y_tiles[r]
-                nc.vector.tensor_tensor(out=y[:, cols], in0=bank[:], in1=y[:, cols], op=ALU.add)
+                for q in quarters:
+                    cols = slice(BANK * q, BANK * (q + 1))
+                    bank = psum.tile([P, BANK], F32, name="r_bank", tag="r", bufs=3)
+                    stage2_bank(bank, r, vw, vs, cols)
+                    nc.vector.tensor_tensor(out=y[:, cols], in0=bank[:], in1=y[:, cols], op=ALU.add)
 
             def finish_z(r):
-                inverse_sigma(r)
-                zo = two.tile([P, J], F32, name="zo")
+                zo = work.tile([P, J], F32, name="zo")
                 nc.scalar.activation(out=zo[:], in_=z_banks[r][:], func=ACT.Copy, scale=inv[r][:])
                 nc.sync.dma_start(out=out_1[P * r : P * (r + 1), :], in_=zo[:])
 
-            def finish_r(eng, r, q):
+            def finish_y(r, engines):
                 y = y_tiles[r]
-                cols = slice(512 * q, 512 * (q + 1))
-                if eng == "s":
-                    nc.scalar.activation(out=y[:, cols], in_=y[:, cols], func=ACT.Copy, scale=inv[r][:])
-                elif eng == "g":
-                    nc.gpsimd.tensor_scalar(
-                        out=y[:, cols], in0=y[:, cols], scalar1=inv[r][:], scalar2=0.0, op0=ALU.mult, op1=ALU.add
-                    )
-                else:
-                    nc.vector.tensor_scalar(
-                        out=y[:, cols], in0=y[:, cols], scalar1=inv[r][:], scalar2=None, op0=ALU.mult
-                    )
+                for q in range(A // BANK):
+                    cols = slice(BANK * q, BANK * (q + 1))
+                    if engines[q] == "s":
+                        nc.scalar.activation(out=y[:, cols], in_=y[:, cols], func=ACT.Copy, scale=inv[r][:])
+                    elif engines[q] == "g":
+                        nc.gpsimd.tensor_scalar(
+                            out=y[:, cols], in0=y[:, cols], scalar1=inv[r][:], scalar2=0.0, op0=ALU.mult, op1=ALU.add
+                        )
+                    else:
+                        nc.vector.tensor_scalar(
+                            out=y[:, cols], in0=y[:, cols], scalar1=inv[r][:], scalar2=None, op0=ALU.mult
+                        )
+                    if q % 2:
+                        pair = slice(BANK * (q - 1), BANK * (q + 1))
+                        nc.sync.dma_start(out=out_0[P * r : P * (r + 1), pair], in_=y[:, pair])
 
-            def store_r(r, half):
-                cols = slice(1024 * half, 1024 * (half + 1))
-                nc.sync.dma_start(out=out_0[P * r : P * (r + 1), cols], in_=y_tiles[r][:, cols])
-
-            def spread_spec(q):
-                cols = slice(512 * q, 512 * (q + 1))
-                bank = psum.tile([P, 512], F32, name="mm_bank", tag="mm", bufs=4)
+            permute_scales(0)
+            permute_words(0)
+            for q in range(4):
+                cols = slice(BANK * q, BANK * (q + 1))
+                bank = psum.tile([P, BANK], F32, name="s_bank", tag="rxxr"[q], bufs=(3, 2, 2, 3)[q])
                 nc.tensor.matmul(bank[:], ones[:], spec_row[:, cols], start=True, stop=True)
                 nc.scalar.copy(out=spec_bc[:, cols], in_=bank[:])
-
-            def stage2(r):
-                for q in range(4):
-                    stage2_r(r, q)
-
-            def tile_out(r, d):
-                for q in range(4):
-                    finish_r(d[q], r, q)
-                store_r(r, 0)
-                store_r(r, 1)
-
-            for q in range(4):
-                spread_spec(q)
-            for vec, raw, factor in ((nbench, bench_in, -0.5), (vol2, vol_in, 2.0)):
-                nc.gpsimd.tensor_scalar(
-                    out=vec[:],
-                    in0=raw[:].rearrange("p e t -> p (e t)"),
-                    scalar1=factor,
-                    scalar2=0.0,
-                    op0=ALU.mult,
-                    op1=ALU.add,
-                )
-            perm_scales()
-            perm_words(0)
-            open_chunk(0)
-            for r in range(4):
-                transposes(r, "xt" if r % 2 == 0 else "z")
-            make_y(nc.vector, 0)
-            for g in range(KH):
-                quantize_h(0, g)
-            square_y(0)
-            make_y(nc.vector, 1)
-
-            open_chunk(1)
-            stage1(0, 0, 0)
-            perm_words(1)
-            stage1(0, 0, 1)
-            transposes(4, "xt")
-            make_y(nc.vector, 2)
-            stage1(0, 0, 2)
-            transposes(5, "xt")
-            stage1(0, 0, 3)
-            transposes(6, "xt")
-            scale_e(0, 0, 0)
-            scale_e(0, 0, 1)
-            stage1(0, 1, 0)
-            transposes(7, "xt")
-            square_y(1)
-            quantize_e(0, 0, None)
-            for g in range(KH):
-                quantize_h(1, g)
-            for t in range(1, 4):
-                stage1(0, 1, t)
-            make_y(nc.vector, 3)
-            for half in range(2):
-                scale_e(0, 1, half)
-            for half in range(2):
-                quantize_e(0, 1, half)
-            square_y(2)
-
-            for t in range(3):
-                stage1(1, 0, t)
-            make_y(nc.vector, 4)
-            stage2_z(0)
-            square_z(0)
-            stage2(0)
-            stage1(1, 0, 3)
-            stage1(1, 1, 0)
-            finish_z(0)
-            scale_e(1, 0, 0)
-            scale_e(1, 0, 1)
-            square_y(3)
-            tile_out(0, "ssss")
-            stage2_z(1)
-            square_z(1)
-            stage2(1)
-            quantize_e(1, 0, None)
-            for t in range(1, 4):
-                stage1(1, 1, t)
-            finish_z(1)
-            make_y(nc.vector, 5)
-            tile_out(1, "ssss")
-            stage2_z(2)
-            for half in range(2):
-                scale_e(1, 1, half)
-            for half in range(2):
-                quantize_e(1, 1, half)
-            square_z(2)
-            finish_z(2)
-            stage2_z(3)
-            stage2(2)
-            square_z(3)
-            for r in range(3, NR):
-                if r + 1 < NR:
-                    stage2_z(r + 1)
-                    square_z(r + 1)
-                stage2(r)
-                if r in (4, 5):
-                    make_y(nc.vector, r + 2)
-                finish_z(r)
-                tile_out(r - 1, "gggg" if r == 6 else "sggg")
-                if r + 1 < NR :
-                    square_y(r + 1)
-            tile_out(NR - 1, "sgvv")
+            nc.gpsimd.tensor_scalar(
+                out=nbench[:], in0=bench_in[:], scalar1=-0.5, scalar2=0.0, op0=ALU.mult, op1=ALU.add
+            )
+            nc.gpsimd.tensor_scalar(
+                out=vol2[:],
+                in0=vol_in[:].unsqueeze(2).to_broadcast([P, GE, P // PACK, PACK]),
+                scalar1=2.0,
+                scalar2=0.0,
+                op0=ALU.mult,
+                op1=ALU.add,
+            )
+            permute_scales(1)
+            for n in range(-3, NR):
+                if n >= 0:
+                    stage2_z(n)
+                    inverse_sigma(n)
+                if n >= 1:
+                    finish_y(n - 1, "sggg")
+                if 0 <= n + 1 < NR:
+                    square_y(n + 1)
+                if 0 <= n + 1 < NR:
+                    scale_e(n + 1)
+                if n >= 0:
+                    stage2_r(n, range(A // BANK))
+                if 0 <= n + 3 < NR:
+                    transpose_h(n + 3)
+                if 0 <= n + 1 < NR:
+                    quantize_e(n + 1)
+                if 0 <= n + 2 < NR:
+                    make_y(n + 2)
+                if n >= 0:
+                    finish_z(n)
+                if n + 3 < NR:
+                    quantize_h(n + 3)
+                if n == -3:
+                    permute_words(1)
+                if 0 <= n + 2 < NR:
+                    stage1(n + 2)
+            finish_y(NR - 1, "ssvv")

@@ -18,10 +18,16 @@ ACT = mybir.ActivationFunctionType
 
 P = 128
 PACK = 4
-KH = A // 512
-GE = F // 512
-NR = M // P
+K_PASS = P * PACK
+ASSET_PASSES = A // K_PASS
+FACTOR_PASSES = F // K_PASS
+TILES = M // P
 BANK = 512
+QUARTERS = A // BANK
+RUN = 4
+
+DIVIDERS = ("scalar", "gpsimd", "gpsimd", "gpsimd")
+LAST_DIVIDERS = ("scalar", "vector", "scalar", "vector")
 
 
 def tile_factor_risk_apply_f7_kernel(
@@ -30,44 +36,54 @@ def tile_factor_risk_apply_f7_kernel(
     nc = tc.nc
     with ExitStack() as ctx:
         keep = ctx.enter_context(tc.tile_pool(name="keep", bufs=1))
-        hpool = ctx.enter_context(tc.tile_pool(name="hpool", bufs=8))
-        ypool = ctx.enter_context(tc.tile_pool(name="ypool", bufs=6))
+        h_pool = ctx.enter_context(tc.tile_pool(name="h_pool", bufs=TILES))
+        y_pool = ctx.enter_context(tc.tile_pool(name="y_pool", bufs=6))
         work = ctx.enter_context(tc.tile_pool(name="work", bufs=3))
-        small = ctx.enter_context(tc.tile_pool(name="small", bufs=8))
-        psum = ctx.enter_context(tc.psum_pool(name="psum", bufs=2))
+        small = ctx.enter_context(tc.tile_pool(name="small", bufs=TILES))
+        psum_t = ctx.enter_context(tc.psum_pool(name="psum_t", bufs=2))
+        psum_x = ctx.enter_context(tc.psum_pool(name="psum_x", bufs=2))
+        psum_z = ctx.enter_context(tc.psum_pool(name="psum_z", bufs=1))
+        psum_r = ctx.enter_context(tc.psum_pool(name="psum_r", bufs=3))
 
         warm = keep.tile([P, 8], F32, name="warm")
-        spec_row = keep.tile([P, A], BF16, name="spec_row")
-        ones = keep.tile([P, P], BF16, name="ones")
         ident = keep.tile([P, P], F32, name="ident")
-        mhalf = keep.tile([P, 1], F32, name="mhalf")
-        spec_bc = keep.tile([P, A], BF16, name="spec_bc")
-        bw_raw = [keep.tile([P, KH, F], U8, name="bw_raw%d" % e, align_bytes=64) for e in range(GE)]
-        bs_raw = keep.tile([P, KH, F], U8, name="bs_raw", align_bytes=64)
-        bw = [keep.tile([P, PACK, KH, 2 * P], U8, name="bw%d" % e, align_bytes=64) for e in range(GE)]
-        bs = [keep.tile([P, PACK, KH, P], U8, name="bs%d" % e, align_bytes=64) for e in range(GE)]
-        lw = keep.tile([P, GE, J], U32, name="lw", align_bytes=64)
-        vw = keep.tile([P, GE, A], U32, name="vw", align_bytes=64)
-        ls = keep.tile([P, GE, J], U8, name="ls", align_bytes=64)
-        vs = keep.tile([P, GE, A], U8, name="vs", align_bytes=64)
-        bench_in = keep.tile([P, GE, PACK], BF16, name="bench_in")
-        vol_in = keep.tile([P, GE, PACK], BF16, name="vol_in")
-        nbench = keep.tile([P, GE, PACK], F32, name="nbench")
-        vol2 = keep.tile([P, GE, P // PACK, PACK], F32, name="vol2")
-        junk = keep.tile([P, A], BF16, name="junk")
+        ones = keep.tile([P, P], BF16, name="ones")
+        minus_half = keep.tile([P, 1], F32, name="minus_half")
+        spec_row = keep.tile([P, A], BF16, name="spec_row")
+        spec_all = keep.tile([P, A], BF16, name="spec_all")
+        bench_in = keep.tile([P, FACTOR_PASSES, PACK], BF16, name="bench_in")
+        vol_in = keep.tile([P, FACTOR_PASSES, PACK], BF16, name="vol_in")
+        tanh_bias = keep.tile([P, FACTOR_PASSES, PACK], F32, name="tanh_bias")
+        cap_vol = keep.tile([P, FACTOR_PASSES, P // RUN, PACK], F32, name="cap_vol")
+        squares = keep.tile([P, A], BF16, name="squares")
 
-        nc.vector.memset(bs_raw[:].rearrange("p g n -> p (g n)").bitcast(I32), 0)
+        b_in = [keep.tile([P, ASSET_PASSES, F], U8, name="b_in%d" % e, align_bytes=64) for e in range(FACTOR_PASSES)]
+        b_scales_in = keep.tile([P, ASSET_PASSES, F], U8, name="b_scales_in", align_bytes=64)
+        b_words = [
+            keep.tile([P, PACK, ASSET_PASSES, 2 * P], U8, name="b_words%d" % e, align_bytes=64)
+            for e in range(FACTOR_PASSES)
+        ]
+        b_scales = [
+            keep.tile([P, PACK, ASSET_PASSES, P], U8, name="b_scales%d" % e, align_bytes=64)
+            for e in range(FACTOR_PASSES)
+        ]
+        l_words = keep.tile([P, FACTOR_PASSES, J], U32, name="l_words", align_bytes=64)
+        l_scales = keep.tile([P, FACTOR_PASSES, J], U8, name="l_scales", align_bytes=64)
+        v_words = keep.tile([P, FACTOR_PASSES, A], U32, name="v_words", align_bytes=64)
+        v_scales = keep.tile([P, FACTOR_PASSES, A], U8, name="v_scales", align_bytes=64)
+        h_tiles = [h_pool.tile([P, A], BF16, name="h_tile", align_bytes=64) for r in range(TILES)]
+
+        nc.vector.memset(b_scales_in[:].rearrange("p g n -> p (g n)").bitcast(I32), 0)
         nc.vector.memset(ones[:], 1.0)
         nc.vector.memset(spec_row[:].bitcast(I32), 0)
         nc.vector.memset(warm[:], 0.0)
         make_identity(nc, ident[:])
-        nc.gpsimd.memset(mhalf[:], -0.5)
-        nc.gpsimd.memset(ls[:].rearrange("p g n -> p (g n)").bitcast(I32), 0)
-        nc.gpsimd.memset(vs[:].rearrange("p g n -> p (g n)").bitcast(I32), 0)
-
-        h_tiles = [hpool.tile([P, A], BF16, name="h", align_bytes=64) for r in range(NR)]
+        nc.gpsimd.memset(minus_half[:], -0.5)
+        nc.gpsimd.memset(l_scales[:].rearrange("p g n -> p (g n)").bitcast(I32), 0)
+        nc.gpsimd.memset(v_scales[:].rearrange("p g n -> p (g n)").bitcast(I32), 0)
 
         with tc.manual_schedule():
+
             def load_scale_rows(dst, src):
                 for quad in range(4):
                     nc.sync.dma_start(
@@ -77,235 +93,273 @@ def tile_factor_risk_apply_f7_kernel(
 
             def load_b_words(e):
                 nc.sync.dma_start(
-                    out=bw_raw[e][:], in_=load_words[:, :, F * e : F * (e + 1)].rearrange("g p b -> p g b")
+                    out=b_in[e][:], in_=load_words[:, :, F * e : F * (e + 1)].rearrange("g p b -> p g b")
                 )
 
             def load_h(r):
                 nc.sync.dma_start(out=h_tiles[r][:], in_=hold[P * r : P * (r + 1), :])
 
-            def load_words_of(dst, src, e):
-                nc.sync.dma_start(out=dst[:, e, :].bitcast(I32), in_=src[e].rearrange("p n t -> p (n t)").bitcast(I32))
+            def load_factor_vector(dst, src):
+                nc.sync.dma_start(out=dst[:], in_=src.rearrange("(e p t) -> p e t", p=P, t=PACK))
 
-            load_scale_rows(bs_raw, load_scales)
+            def load_fp8_words(dst, src):
+                for e in range(FACTOR_PASSES):
+                    nc.sync.dma_start(
+                        out=dst[:, e, :].bitcast(I32), in_=src[e].rearrange("p n t -> p (n t)").bitcast(I32)
+                    )
+
+            load_scale_rows(b_scales_in, load_scales)
             load_b_words(0)
             nc.sync.dma_start(out=spec_row[0:1, :], in_=spec.rearrange("(o n) -> o n", o=1))
             load_h(0)
             load_b_words(1)
             load_h(1)
-            nc.sync.dma_start(out=bench_in[:], in_=bench.rearrange("(e p t) -> p e t", p=P, t=PACK))
-            nc.sync.dma_start(out=vol_in[:], in_=vol.rearrange("(e p t) -> p e t", p=P, t=PACK))
+            load_factor_vector(bench_in, bench)
+            load_factor_vector(vol_in, vol)
             load_h(2)
-            load_scale_rows(ls, mix_scales)
-            load_scale_rows(vs, cov_scales)
-            for e in range(GE):
-                load_words_of(lw, mix_words, e)
-            for e in range(GE):
-                load_words_of(vw, cov_words, e)
-            for r in range(3, NR):
+            load_scale_rows(l_scales, mix_scales)
+            load_scale_rows(v_scales, cov_scales)
+            load_fp8_words(l_words, mix_words)
+            load_fp8_words(v_words, cov_words)
+            for r in range(3, TILES):
                 load_h(r)
 
             nc.scalar.activation(out=warm[:, 0:1], in_=warm[:, 1:2], func=ACT.Tanh)
 
-            def permute_words(e):
+            def order_b_scales(e):
+                half = b_scales_in[:, :, K_PASS * e : K_PASS * (e + 1)]
                 nc.vector.tensor_copy(
-                    out=bw[e][:].rearrange("p t g (m b) -> p t (g m) b", b=2),
-                    in_=bw_raw[e][:].rearrange("p g (m t b) -> p t (g m) b", t=PACK, b=2),
+                    out=b_scales[e][:].rearrange("p t g m -> p g t m"),
+                    in_=half.rearrange("p g (m t) -> p g t m", t=PACK),
                 )
 
-            def permute_scales(e):
+            def order_b_words(e):
                 nc.vector.tensor_copy(
-                    out=bs[e][:].rearrange("p t g m -> p g t m"),
-                    in_=bs_raw[:, :, BANK * e : BANK * (e + 1)].rearrange("p g (m t) -> p g t m", t=PACK),
+                    out=b_words[e][:].rearrange("p t g (m b) -> p t (g m) b", b=2),
+                    in_=b_in[e][:].rearrange("p g (m t b) -> p t (g m) b", t=PACK, b=2),
                 )
 
-            grouped, h_codes, x_raw, e_grouped, e_codes = {}, {}, {}, {}, {}
-            y_tiles, sums, inv, z_banks = {}, {}, {}, {}
+            order_b_scales(0)
+            order_b_words(0)
 
-            def transpose_h(r):
-                words = h_tiles[r][:].bitcast(F32)
-                grp = work.tile([P, KH, P, PACK], BF16, name="grp", align_bytes=64)
-                grouped[r] = grp
-                for half in range(2):
-                    bank = psum.tile([P, 2, 2, P], F32, name="xt_bank", tag="xt", bufs=2)
-                    for gg in range(2):
-                        g = 2 * half + gg
-                        for u in range(2):
-                            nc.tensor.transpose(
-                                bank[:, gg, u, :], words[:, 256 * g + u : 256 * (g + 1) : 2], ident[:]
-                            )
-                    nc.scalar.copy(
-                        out=grp[:, 2 * half : 2 * half + 2, :, :].bitcast(F32),
-                        in_=bank[:].rearrange("p g u r -> p g r u"),
-                    )
-
-            def quantize_h(r):
-                hq = work.tile([P, KH, P], U32, name="hq", align_bytes=64)
-                hs = work.tile([P, KH, P], U8, name="hs", align_bytes=64)
-                h_codes[r] = (hq, hs)
-                nc.vector.quantize_mx(
-                    out=hq[:].rearrange("p g r -> p (g r)").bitcast(FP8X4),
-                    scales=hs[:].rearrange("p g r -> p (g r)"),
-                    in_=grouped[r][:].rearrange("p g r t -> p (g r t)"),
-                )
-
-            def make_y(r):
-                y = ypool.tile([P, A], F32, name="y")
-                y_tiles[r] = y
-                nc.vector.tensor_tensor(out=y[:], in0=h_tiles[r][:], in1=spec_bc[:], op=ALU.mult)
-
-            def square_y(r):
-                s = small.tile([P, 1], F32, name="sum_y")
-                sums[r] = [s]
-                nc.scalar.activation(out=junk[:], in_=y_tiles[r][:], func=ACT.Square, scale=A**-0.5, accum_out=s[:])
-
-            def stage1(r):
-                xr = work.tile([P, PACK, GE, P], F32, name="xr")
-                x_raw[r] = xr
-                hq, hs = h_codes[r]
-                for e in range(GE):
-                    bank = psum.tile([P, PACK, P], F32, name="x_bank", tag="x", bufs=2)
-                    for t in range(PACK):
-                        for g in range(KH):
-                            nc.tensor.matmul_mx(
-                                out=bank[:, t, :],
-                                lhsT=bw[e][:, t, g, :].bitcast(FP4X4),
-                                lhsT_scale=bs[e][:, t, g, :],
-                                rhs=hq[:, g, :].bitcast(FP8X4),
-                                rhs_scale=hs[:, g, :],
-                                start=(g == 0),
-                                stop=(g == KH - 1),
-                            )
-                    for t in range(PACK):
-                        nc.scalar.activation(
-                            out=xr[:, t, e, :],
-                            in_=bank[:, t, :],
-                            func=ACT.Tanh,
-                            bias=nbench[:, e, t : t + 1],
-                            scale=0.5,
-                        )
-
-            def scale_e(r):
-                eg = work.tile([P, GE, P, PACK], BF16, name="eg", align_bytes=64)
-                e_grouped[r] = eg
-                nc.vector.tensor_tensor(
-                    out=eg[:].rearrange("p e (n i) t -> p (e n) t i", i=4),
-                    in0=x_raw[r][:].rearrange("p t e (n i) -> p (e n) t i", i=4),
-                    in1=vol2[:].rearrange("p e n t -> p (e n) t").unsqueeze(3).to_broadcast([P, GE * P // 4, PACK, 4]),
-                    op=ALU.mult,
-                )
-
-            def quantize_e(r):
-                eq = work.tile([P, GE, P], U32, name="eq", align_bytes=64)
-                es = work.tile([P, GE, P], U8, name="es", align_bytes=64)
-                e_codes[r] = (eq, es)
-                nc.vector.quantize_mx(
-                    out=eq[:].rearrange("p e n -> p (e n)").bitcast(FP8X4),
-                    scales=es[:].rearrange("p e n -> p (e n)"),
-                    in_=e_grouped[r][:].rearrange("p e n t -> p (e n t)"),
-                )
-
-            def stage2_bank(bank, r, w, s, cols):
-                eq, es = e_codes[r]
-                for e in range(GE):
-                    nc.tensor.matmul_mx(
-                        out=bank[:],
-                        lhsT=eq[:, e, :].bitcast(FP8X4),
-                        lhsT_scale=es[:, e, :],
-                        rhs=w[:, e, cols].bitcast(FP8X4),
-                        rhs_scale=s[:, e, cols],
-                        start=(e == 0),
-                        stop=(e == GE - 1),
-                    )
-
-            def stage2_z(r):
-                bank = psum.tile([P, J], F32, name="z_bank", tag="z", bufs=1)
-                z_banks[r] = bank
-                stage2_bank(bank, r, lw, ls, slice(0, J))
-                s = small.tile([P, 1], F32, name="sum_z")
-                sums[r].append(s)
-                nc.scalar.activation(out=junk[:, 0:J], in_=bank[:], func=ACT.Square, scale=J**-0.5, accum_out=s[:])
-
-            def inverse_sigma(r):
-                var = small.tile([P, 1], F32, name="var")
-                nc.gpsimd.tensor_tensor(out=var[:], in0=sums[r][0][:], in1=sums[r][1][:], op=ALU.add)
-                inv_t = small.tile([P, 1], F32, name="inv_t")
-                nc.gpsimd.tensor_tensor(out=inv_t[:], in0=var[:], in1=mhalf[:], op=ALU.pow)
-                inv[r] = inv_t
-
-            def stage2_r(r, quarters):
-                y = y_tiles[r]
-                for q in quarters:
-                    cols = slice(BANK * q, BANK * (q + 1))
-                    bank = psum.tile([P, BANK], F32, name="r_bank", tag="r", bufs=3)
-                    stage2_bank(bank, r, vw, vs, cols)
-                    nc.vector.tensor_tensor(out=y[:, cols], in0=bank[:], in1=y[:, cols], op=ALU.add)
-
-            def finish_z(r):
-                zo = work.tile([P, J], F32, name="zo")
-                nc.scalar.activation(out=zo[:], in_=z_banks[r][:], func=ACT.Copy, scale=inv[r][:])
-                nc.sync.dma_start(out=out_1[P * r : P * (r + 1), :], in_=zo[:])
-
-            def finish_y(r, engines):
-                y = y_tiles[r]
-                for q in range(A // BANK):
-                    cols = slice(BANK * q, BANK * (q + 1))
-                    if engines[q] == "s":
-                        nc.scalar.activation(out=y[:, cols], in_=y[:, cols], func=ACT.Copy, scale=inv[r][:])
-                    elif engines[q] == "g":
-                        nc.gpsimd.tensor_scalar(
-                            out=y[:, cols], in0=y[:, cols], scalar1=inv[r][:], scalar2=0.0, op0=ALU.mult, op1=ALU.add
-                        )
-                    else:
-                        nc.vector.tensor_scalar(
-                            out=y[:, cols], in0=y[:, cols], scalar1=inv[r][:], scalar2=None, op0=ALU.mult
-                        )
-                    if q % 2:
-                        pair = slice(BANK * (q - 1), BANK * (q + 1))
-                        nc.sync.dma_start(out=out_0[P * r : P * (r + 1), pair], in_=y[:, pair])
-
-            permute_scales(0)
-            permute_words(0)
-            for q in range(4):
+            for q in range(QUARTERS):
                 cols = slice(BANK * q, BANK * (q + 1))
-                bank = psum.tile([P, BANK], F32, name="s_bank", tag="rxxr"[q], bufs=(3, 2, 2, 3)[q])
+                if q in (0, 3):
+                    bank = psum_r.tile([P, BANK], F32, name="r_bank")
+                else:
+                    bank = psum_x.tile([P, BANK], F32, name="x_bank")
                 nc.tensor.matmul(bank[:], ones[:], spec_row[:, cols], start=True, stop=True)
-                nc.scalar.copy(out=spec_bc[:, cols], in_=bank[:])
+                nc.scalar.copy(out=spec_all[:, cols], in_=bank[:])
+
             nc.gpsimd.tensor_scalar(
-                out=nbench[:], in0=bench_in[:], scalar1=-0.5, scalar2=0.0, op0=ALU.mult, op1=ALU.add
+                out=tanh_bias[:], in0=bench_in[:], scalar1=-0.5, scalar2=0.0, op0=ALU.mult, op1=ALU.add
             )
             nc.gpsimd.tensor_scalar(
-                out=vol2[:],
-                in0=vol_in[:].unsqueeze(2).to_broadcast([P, GE, P // PACK, PACK]),
+                out=cap_vol[:],
+                in0=vol_in[:].unsqueeze(2).to_broadcast([P, FACTOR_PASSES, P // RUN, PACK]),
                 scalar1=2.0,
                 scalar2=0.0,
                 op0=ALU.mult,
                 op1=ALU.add,
             )
-            permute_scales(1)
-            for n in range(-3, NR):
-                if n >= 0:
-                    stage2_z(n)
-                    inverse_sigma(n)
-                if n >= 1:
-                    finish_y(n - 1, "sggg")
-                if 0 <= n + 1 < NR:
-                    square_y(n + 1)
-                if 0 <= n + 1 < NR:
-                    scale_e(n + 1)
-                if n >= 0:
-                    stage2_r(n, range(A // BANK))
-                if 0 <= n + 3 < NR:
-                    transpose_h(n + 3)
-                if 0 <= n + 1 < NR:
-                    quantize_e(n + 1)
-                if 0 <= n + 2 < NR:
-                    make_y(n + 2)
-                if n >= 0:
-                    finish_z(n)
-                if n + 3 < NR:
-                    quantize_h(n + 3)
-                if n == -3:
-                    permute_words(1)
-                if 0 <= n + 2 < NR:
-                    stage1(n + 2)
-            finish_y(NR - 1, "ssvv")
+            order_b_scales(1)
+            order_b_words(1)
+
+            t_banks, x_banks, z_banks, r_banks = {}, {}, {}, {}
+            h_groups, h_codes, caps, e_groups, e_codes = {}, {}, {}, {}, {}
+            y_tiles, z_tiles, sum_y, sum_z, inverse = {}, {}, {}, {}, {}
+
+            def transpose_h(r, half):
+                words = h_tiles[r][:].bitcast(F32)
+                bank = psum_t.tile([P, 2, 2, P], F32, name="t_bank")
+                t_banks[r, half] = bank
+                for i in range(2):
+                    first = (2 * half + i) * K_PASS // 2
+                    for u in range(2):
+                        nc.tensor.transpose(bank[:, i, u, :], words[:, first + u : first + K_PASS // 2 : 2], ident[:])
+
+            def copy_h(r, half):
+                if half == 0:
+                    group = work.tile([P, ASSET_PASSES, P, PACK], BF16, name="group", align_bytes=64)
+                    h_groups[r] = group
+                nc.scalar.copy(
+                    out=h_groups[r][:, 2 * half : 2 * half + 2, :, :].bitcast(F32),
+                    in_=t_banks[r, half][:].rearrange("p i u n -> p i n u"),
+                )
+
+            def quantize_h(r):
+                words = work.tile([P, ASSET_PASSES, P], U32, name="h_word", align_bytes=64)
+                scales = work.tile([P, ASSET_PASSES, P], U8, name="h_scale", align_bytes=64)
+                h_codes[r] = (words, scales)
+                nc.vector.quantize_mx(
+                    out=words[:].rearrange("p g n -> p (g n)").bitcast(FP8X4),
+                    scales=scales[:].rearrange("p g n -> p (g n)"),
+                    in_=h_groups[r][:].rearrange("p g n t -> p (g n t)"),
+                )
+
+            def stage1(r, e):
+                words, scales = h_codes[r]
+                bank = psum_x.tile([P, PACK, P], F32, name="x_bank")
+                x_banks[r, e] = bank
+                for t in range(PACK):
+                    for g in range(ASSET_PASSES):
+                        nc.tensor.matmul_mx(
+                            out=bank[:, t, :],
+                            lhsT=b_words[e][:, t, g, :].bitcast(FP4X4),
+                            lhsT_scale=b_scales[e][:, t, g, :],
+                            rhs=words[:, g, :].bitcast(FP8X4),
+                            rhs_scale=scales[:, g, :],
+                            start=(g == 0),
+                            stop=(g == ASSET_PASSES - 1),
+                        )
+
+            def cap(r, e):
+                if e == 0:
+                    capped = work.tile([P, PACK, FACTOR_PASSES, P], F32, name="capped")
+                    caps[r] = capped
+                for t in range(PACK):
+                    nc.scalar.activation(
+                        out=caps[r][:, t, e, :],
+                        in_=x_banks[r, e][:, t, :],
+                        func=ACT.Tanh,
+                        bias=tanh_bias[:, e, t : t + 1],
+                        scale=0.5,
+                    )
+
+            def scale_e(r):
+                group = work.tile([P, FACTOR_PASSES, P, PACK], BF16, name="e_group", align_bytes=64)
+                e_groups[r] = group
+                runs = FACTOR_PASSES * P // RUN
+                nc.vector.tensor_tensor(
+                    out=group[:].rearrange("p e (n i) t -> p (e n) t i", i=RUN),
+                    in0=caps[r][:].rearrange("p t e (n i) -> p (e n) t i", i=RUN),
+                    in1=cap_vol[:]
+                    .rearrange("p e n t -> p (e n) t")
+                    .unsqueeze(3)
+                    .to_broadcast([P, runs, PACK, RUN]),
+                    op=ALU.mult,
+                )
+
+            def quantize_e(r):
+                words = work.tile([P, FACTOR_PASSES, P], U32, name="e_word", align_bytes=64)
+                scales = work.tile([P, FACTOR_PASSES, P], U8, name="e_scale", align_bytes=64)
+                e_codes[r] = (words, scales)
+                nc.vector.quantize_mx(
+                    out=words[:].rearrange("p e n -> p (e n)").bitcast(FP8X4),
+                    scales=scales[:].rearrange("p e n -> p (e n)"),
+                    in_=e_groups[r][:].rearrange("p e n t -> p (e n t)"),
+                )
+
+            def stage2(bank, r, weight_words, weight_scales, cols):
+                words, scales = e_codes[r]
+                for e in range(FACTOR_PASSES):
+                    nc.tensor.matmul_mx(
+                        out=bank[:],
+                        lhsT=words[:, e, :].bitcast(FP8X4),
+                        lhsT_scale=scales[:, e, :],
+                        rhs=weight_words[:, e, cols].bitcast(FP8X4),
+                        rhs_scale=weight_scales[:, e, cols],
+                        start=(e == 0),
+                        stop=(e == FACTOR_PASSES - 1),
+                    )
+
+            def stage2_z(r):
+                bank = psum_z.tile([P, J], F32, name="z_bank")
+                z_banks[r] = bank
+                stage2(bank, r, l_words, l_scales, slice(0, J))
+
+            def stage2_r(r, q):
+                bank = psum_r.tile([P, BANK], F32, name="r_bank")
+                r_banks[r, q] = bank
+                stage2(bank, r, v_words, v_scales, slice(BANK * q, BANK * (q + 1)))
+
+            def make_y(r):
+                y = y_pool.tile([P, A], F32, name="y")
+                y_tiles[r] = y
+                nc.vector.tensor_tensor(out=y[:], in0=h_tiles[r][:], in1=spec_all[:], op=ALU.mult)
+
+            def square_y(r):
+                total = small.tile([P, 1], F32, name="total_y")
+                sum_y[r] = total
+                nc.scalar.activation(
+                    out=squares[:], in_=y_tiles[r][:], func=ACT.Square, scale=A**-0.5, accum_out=total[:]
+                )
+
+            def square_z(r):
+                total = small.tile([P, 1], F32, name="total_z")
+                sum_z[r] = total
+                nc.scalar.activation(
+                    out=squares[:, 0:J], in_=z_banks[r][:], func=ACT.Square, scale=J**-0.5, accum_out=total[:]
+                )
+
+            def invert_sigma(r):
+                variance = small.tile([P, 1], F32, name="variance")
+                nc.gpsimd.tensor_tensor(out=variance[:], in0=sum_y[r][:], in1=sum_z[r][:], op=ALU.add)
+                factor = small.tile([P, 1], F32, name="factor")
+                nc.gpsimd.tensor_tensor(out=factor[:], in0=variance[:], in1=minus_half[:], op=ALU.pow)
+                inverse[r] = factor
+
+            def divide_z(r):
+                z = work.tile([P, J], F32, name="z")
+                z_tiles[r] = z
+                nc.scalar.activation(out=z[:], in_=z_banks[r][:], func=ACT.Copy, scale=inverse[r][:])
+
+            def store_z(r):
+                nc.sync.dma_start(out=out_1[P * r : P * (r + 1), :], in_=z_tiles[r][:])
+
+            def add_y(r, q):
+                y = y_tiles[r][:, BANK * q : BANK * (q + 1)]
+                nc.vector.tensor_tensor(out=y, in0=r_banks[r, q][:], in1=y, op=ALU.add)
+
+            def divide_y(r, q):
+                y = y_tiles[r][:, BANK * q : BANK * (q + 1)]
+                engine = (LAST_DIVIDERS if r == TILES - 1 else DIVIDERS)[q]
+                if engine == "scalar":
+                    nc.scalar.activation(out=y, in_=y, func=ACT.Copy, scale=inverse[r][:])
+                elif engine == "gpsimd":
+                    nc.gpsimd.tensor_scalar(
+                        out=y, in0=y, scalar1=inverse[r][:], scalar2=0.0, op0=ALU.mult, op1=ALU.add
+                    )
+                else:
+                    nc.vector.tensor_scalar(out=y, in0=y, scalar1=inverse[r][:], scalar2=None, op0=ALU.mult)
+
+            def store_y(r, half):
+                cols = slice(2 * BANK * half, 2 * BANK * (half + 1))
+                nc.sync.dma_start(out=out_0[P * r : P * (r + 1), cols], in_=y_tiles[r][:, cols])
+
+            def run(step, r, *which):
+                if 0 <= r < TILES:
+                    step(r, *which)
+
+            for n in range(-3, TILES + 1):
+                run(stage2_z, n)
+                run(add_y, n - 1, 2)
+                run(stage2_r, n, 0)
+                run(quantize_h, n + 2)
+                run(divide_y, n - 1, 0)
+                run(stage2_r, n, 1)
+                run(divide_y, n - 1, 1)
+                run(store_y, n - 1, 0)
+                run(add_y, n - 1, 3)
+                for half in range(2):
+                    run(transpose_h, n + 3, half)
+                    run(cap, n + 1, half)
+                run(divide_y, n - 1, 2)
+                run(stage2_r, n, 2)
+                run(scale_e, n + 1)
+                run(add_y, n, 0)
+                run(divide_y, n - 1, 3)
+                run(store_y, n - 1, 1)
+                run(quantize_e, n + 1)
+                run(square_z, n)
+                run(stage1, n + 2, 0)
+                run(invert_sigma, n)
+                run(stage2_r, n, 3)
+                run(stage1, n + 2, 1)
+                run(square_y, n + 1)
+                run(divide_z, n)
+                run(store_z, n)
+                run(copy_h, n + 3, 0)
+                run(add_y, n, 1)
+                run(copy_h, n + 3, 1)
+                run(make_y, n + 2)

from contextlib import ExitStack

import concourse.mybir as mybir
from concourse.masks import make_identity

M, A, F, J = 1024, 2048, 1024, 512
FLOPS = 2 * M * A * F + 2 * M * F * (A + J)

F32 = mybir.dt.float32
BF16 = mybir.dt.bfloat16
U32 = mybir.dt.uint32
I32 = mybir.dt.int32
U8 = mybir.dt.uint8
FP8X4 = mybir.dt.float8_e4m3fn_x4
FP4X4 = mybir.dt.float4_e2m1fn_x4
ALU = mybir.AluOpType
ACT = mybir.ActivationFunctionType

P = 128
PACK = 4
K_PASS = P * PACK
ASSET_PASSES = A // K_PASS
FACTOR_PASSES = F // K_PASS
TILES = M // P
BANK = 512
QUARTERS = A // BANK
RUN = 4

DIVIDERS = ("scalar", "gpsimd", "gpsimd", "gpsimd")
LAST_DIVIDERS = ("scalar", "vector", "scalar", "vector")


def tile_factor_risk_apply_f7_kernel(
    tc, hold, load_words, load_scales, bench, vol, mix_words, mix_scales, cov_words, cov_scales, spec, out_0, out_1
):
    nc = tc.nc
    with ExitStack() as ctx:
        keep = ctx.enter_context(tc.tile_pool(name="keep", bufs=1))
        h_pool = ctx.enter_context(tc.tile_pool(name="h_pool", bufs=TILES))
        y_pool = ctx.enter_context(tc.tile_pool(name="y_pool", bufs=6))
        work = ctx.enter_context(tc.tile_pool(name="work", bufs=3))
        small = ctx.enter_context(tc.tile_pool(name="small", bufs=TILES))
        psum_t = ctx.enter_context(tc.psum_pool(name="psum_t", bufs=2))
        psum_x = ctx.enter_context(tc.psum_pool(name="psum_x", bufs=2))
        psum_z = ctx.enter_context(tc.psum_pool(name="psum_z", bufs=1))
        psum_r = ctx.enter_context(tc.psum_pool(name="psum_r", bufs=3))

        warm = keep.tile([P, 8], F32, name="warm")
        ident = keep.tile([P, P], F32, name="ident")
        ones = keep.tile([P, P], BF16, name="ones")
        minus_half = keep.tile([P, 1], F32, name="minus_half")
        spec_row = keep.tile([P, A], BF16, name="spec_row")
        spec_all = keep.tile([P, A], BF16, name="spec_all")
        bench_in = keep.tile([P, FACTOR_PASSES, PACK], BF16, name="bench_in")
        vol_in = keep.tile([P, FACTOR_PASSES, PACK], BF16, name="vol_in")
        tanh_bias = keep.tile([P, FACTOR_PASSES, PACK], F32, name="tanh_bias")
        cap_vol = keep.tile([P, FACTOR_PASSES, P // RUN, PACK], F32, name="cap_vol")
        squares = keep.tile([P, A], BF16, name="squares")

        b_in = [keep.tile([P, ASSET_PASSES, F], U8, name="b_in%d" % e, align_bytes=64) for e in range(FACTOR_PASSES)]
        b_scales_in = keep.tile([P, ASSET_PASSES, F], U8, name="b_scales_in", align_bytes=64)
        b_words = [
            keep.tile([P, PACK, ASSET_PASSES, 2 * P], U8, name="b_words%d" % e, align_bytes=64)
            for e in range(FACTOR_PASSES)
        ]
        b_scales = [
            keep.tile([P, PACK, ASSET_PASSES, P], U8, name="b_scales%d" % e, align_bytes=64)
            for e in range(FACTOR_PASSES)
        ]
        l_words = keep.tile([P, FACTOR_PASSES, J], U32, name="l_words", align_bytes=64)
        l_scales = keep.tile([P, FACTOR_PASSES, J], U8, name="l_scales", align_bytes=64)
        v_words = keep.tile([P, FACTOR_PASSES, A], U32, name="v_words", align_bytes=64)
        v_scales = keep.tile([P, FACTOR_PASSES, A], U8, name="v_scales", align_bytes=64)
        h_tiles = [h_pool.tile([P, A], BF16, name="h_tile", align_bytes=64) for r in range(TILES)]

        nc.vector.memset(b_scales_in[:].rearrange("p g n -> p (g n)").bitcast(I32), 0)
        nc.vector.memset(ones[:], 1.0)
        nc.vector.memset(spec_row[:].bitcast(I32), 0)
        nc.vector.memset(warm[:], 0.0)
        make_identity(nc, ident[:])
        nc.gpsimd.memset(minus_half[:], -0.5)
        nc.gpsimd.memset(l_scales[:].rearrange("p g n -> p (g n)").bitcast(I32), 0)
        nc.gpsimd.memset(v_scales[:].rearrange("p g n -> p (g n)").bitcast(I32), 0)

        with tc.manual_schedule():

            def load_scale_rows(dst, src):
                for quad in range(4):
                    nc.sync.dma_start(
                        out=dst[32 * quad : 32 * quad + 4, :, :].bitcast(I32),
                        in_=src.bitcast(I32)[:, 4 * quad : 4 * quad + 4, :].rearrange("g q n -> q g n"),
                    )

            def load_b_words(e):
                nc.sync.dma_start(
                    out=b_in[e][:], in_=load_words[:, :, F * e : F * (e + 1)].rearrange("g p b -> p g b")
                )

            def load_h(r):
                nc.sync.dma_start(out=h_tiles[r][:], in_=hold[P * r : P * (r + 1), :])

            def load_factor_vector(dst, src):
                nc.sync.dma_start(out=dst[:], in_=src.rearrange("(e p t) -> p e t", p=P, t=PACK))

            def load_fp8_words(dst, src):
                for e in range(FACTOR_PASSES):
                    nc.sync.dma_start(
                        out=dst[:, e, :].bitcast(I32), in_=src[e].rearrange("p n t -> p (n t)").bitcast(I32)
                    )

            load_scale_rows(b_scales_in, load_scales)
            load_b_words(0)
            nc.sync.dma_start(out=spec_row[0:1, :], in_=spec.rearrange("(o n) -> o n", o=1))
            load_h(0)
            load_b_words(1)
            load_h(1)
            load_factor_vector(bench_in, bench)
            load_factor_vector(vol_in, vol)
            load_h(2)
            load_scale_rows(l_scales, mix_scales)
            load_scale_rows(v_scales, cov_scales)
            load_fp8_words(l_words, mix_words)
            load_fp8_words(v_words, cov_words)
            for r in range(3, TILES):
                load_h(r)

            nc.scalar.activation(out=warm[:, 0:1], in_=warm[:, 1:2], func=ACT.Tanh)

            def order_b_scales(e):
                half = b_scales_in[:, :, K_PASS * e : K_PASS * (e + 1)]
                nc.vector.tensor_copy(
                    out=b_scales[e][:].rearrange("p t g m -> p g t m"),
                    in_=half.rearrange("p g (m t) -> p g t m", t=PACK),
                )

            def order_b_words(e):
                nc.vector.tensor_copy(
                    out=b_words[e][:].rearrange("p t g (m b) -> p t (g m) b", b=2),
                    in_=b_in[e][:].rearrange("p g (m t b) -> p t (g m) b", t=PACK, b=2),
                )

            order_b_scales(0)
            order_b_words(0)

            for q in range(QUARTERS):
                cols = slice(BANK * q, BANK * (q + 1))
                if q in (0, 3):
                    bank = psum_r.tile([P, BANK], F32, name="r_bank")
                else:
                    bank = psum_x.tile([P, BANK], F32, name="x_bank")
                nc.tensor.matmul(bank[:], ones[:], spec_row[:, cols], start=True, stop=True)
                nc.scalar.copy(out=spec_all[:, cols], in_=bank[:])

            nc.gpsimd.tensor_scalar(
                out=tanh_bias[:], in0=bench_in[:], scalar1=-0.5, scalar2=0.0, op0=ALU.mult, op1=ALU.add
            )
            nc.gpsimd.tensor_scalar(
                out=cap_vol[:],
                in0=vol_in[:].unsqueeze(2).to_broadcast([P, FACTOR_PASSES, P // RUN, PACK]),
                scalar1=2.0,
                scalar2=0.0,
                op0=ALU.mult,
                op1=ALU.add,
            )
            order_b_scales(1)
            order_b_words(1)

            t_banks, x_banks, z_banks, r_banks = {}, {}, {}, {}
            h_groups, h_codes, caps, e_groups, e_codes = {}, {}, {}, {}, {}
            y_tiles, z_tiles, sum_y, sum_z, inverse = {}, {}, {}, {}, {}

            def transpose_h(r, half):
                words = h_tiles[r][:].bitcast(F32)
                bank = psum_t.tile([P, 2, 2, P], F32, name="t_bank")
                t_banks[r, half] = bank
                for i in range(2):
                    first = (2 * half + i) * K_PASS // 2
                    for u in range(2):
                        nc.tensor.transpose(bank[:, i, u, :], words[:, first + u : first + K_PASS // 2 : 2], ident[:])

            def copy_h(r, half):
                if half == 0:
                    group = work.tile([P, ASSET_PASSES, P, PACK], BF16, name="group", align_bytes=64)
                    h_groups[r] = group
                nc.scalar.copy(
                    out=h_groups[r][:, 2 * half : 2 * half + 2, :, :].bitcast(F32),
                    in_=t_banks[r, half][:].rearrange("p i u n -> p i n u"),
                )

            def quantize_h(r):
                words = work.tile([P, ASSET_PASSES, P], U32, name="h_word", align_bytes=64)
                scales = work.tile([P, ASSET_PASSES, P], U8, name="h_scale", align_bytes=64)
                h_codes[r] = (words, scales)
                nc.vector.quantize_mx(
                    out=words[:].rearrange("p g n -> p (g n)").bitcast(FP8X4),
                    scales=scales[:].rearrange("p g n -> p (g n)"),
                    in_=h_groups[r][:].rearrange("p g n t -> p (g n t)"),
                )

            def stage1(r, e):
                words, scales = h_codes[r]
                bank = psum_x.tile([P, PACK, P], F32, name="x_bank")
                x_banks[r, e] = bank
                for t in range(PACK):
                    for g in range(ASSET_PASSES):
                        nc.tensor.matmul_mx(
                            out=bank[:, t, :],
                            lhsT=b_words[e][:, t, g, :].bitcast(FP4X4),
                            lhsT_scale=b_scales[e][:, t, g, :],
                            rhs=words[:, g, :].bitcast(FP8X4),
                            rhs_scale=scales[:, g, :],
                            start=(g == 0),
                            stop=(g == ASSET_PASSES - 1),
                        )

            def cap(r, e):
                if e == 0:
                    capped = work.tile([P, PACK, FACTOR_PASSES, P], F32, name="capped")
                    caps[r] = capped
                for t in range(PACK):
                    nc.scalar.activation(
                        out=caps[r][:, t, e, :],
                        in_=x_banks[r, e][:, t, :],
                        func=ACT.Tanh,
                        bias=tanh_bias[:, e, t : t + 1],
                        scale=0.5,
                    )

            def scale_e(r):
                group = work.tile([P, FACTOR_PASSES, P, PACK], BF16, name="e_group", align_bytes=64)
                e_groups[r] = group
                runs = FACTOR_PASSES * P // RUN
                nc.vector.tensor_tensor(
                    out=group[:].rearrange("p e (n i) t -> p (e n) t i", i=RUN),
                    in0=caps[r][:].rearrange("p t e (n i) -> p (e n) t i", i=RUN),
                    in1=cap_vol[:]
                    .rearrange("p e n t -> p (e n) t")
                    .unsqueeze(3)
                    .to_broadcast([P, runs, PACK, RUN]),
                    op=ALU.mult,
                )

            def quantize_e(r):
                words = work.tile([P, FACTOR_PASSES, P], U32, name="e_word", align_bytes=64)
                scales = work.tile([P, FACTOR_PASSES, P], U8, name="e_scale", align_bytes=64)
                e_codes[r] = (words, scales)
                nc.vector.quantize_mx(
                    out=words[:].rearrange("p e n -> p (e n)").bitcast(FP8X4),
                    scales=scales[:].rearrange("p e n -> p (e n)"),
                    in_=e_groups[r][:].rearrange("p e n t -> p (e n t)"),
                )

            def stage2(bank, r, weight_words, weight_scales, cols):
                words, scales = e_codes[r]
                for e in range(FACTOR_PASSES):
                    nc.tensor.matmul_mx(
                        out=bank[:],
                        lhsT=words[:, e, :].bitcast(FP8X4),
                        lhsT_scale=scales[:, e, :],
                        rhs=weight_words[:, e, cols].bitcast(FP8X4),
                        rhs_scale=weight_scales[:, e, cols],
                        start=(e == 0),
                        stop=(e == FACTOR_PASSES - 1),
                    )

            def stage2_z(r):
                bank = psum_z.tile([P, J], F32, name="z_bank")
                z_banks[r] = bank
                stage2(bank, r, l_words, l_scales, slice(0, J))

            def stage2_r(r, q):
                bank = psum_r.tile([P, BANK], F32, name="r_bank")
                r_banks[r, q] = bank
                stage2(bank, r, v_words, v_scales, slice(BANK * q, BANK * (q + 1)))

            def make_y(r):
                y = y_pool.tile([P, A], F32, name="y")
                y_tiles[r] = y
                nc.vector.tensor_tensor(out=y[:], in0=h_tiles[r][:], in1=spec_all[:], op=ALU.mult)

            def square_y(r):
                total = small.tile([P, 1], F32, name="total_y")
                sum_y[r] = total
                nc.scalar.activation(
                    out=squares[:], in_=y_tiles[r][:], func=ACT.Square, scale=A**-0.5, accum_out=total[:]
                )

            def square_z(r):
                total = small.tile([P, 1], F32, name="total_z")
                sum_z[r] = total
                nc.scalar.activation(
                    out=squares[:, 0:J], in_=z_banks[r][:], func=ACT.Square, scale=J**-0.5, accum_out=total[:]
                )

            def invert_sigma(r):
                variance = small.tile([P, 1], F32, name="variance")
                nc.gpsimd.tensor_tensor(out=variance[:], in0=sum_y[r][:], in1=sum_z[r][:], op=ALU.add)
                factor = small.tile([P, 1], F32, name="factor")
                nc.gpsimd.tensor_tensor(out=factor[:], in0=variance[:], in1=minus_half[:], op=ALU.pow)
                inverse[r] = factor

            def divide_z(r):
                z = work.tile([P, J], F32, name="z")
                z_tiles[r] = z
                nc.scalar.activation(out=z[:], in_=z_banks[r][:], func=ACT.Copy, scale=inverse[r][:])

            def store_z(r):
                nc.sync.dma_start(out=out_1[P * r : P * (r + 1), :], in_=z_tiles[r][:])

            def add_y(r, q):
                y = y_tiles[r][:, BANK * q : BANK * (q + 1)]
                nc.vector.tensor_tensor(out=y, in0=r_banks[r, q][:], in1=y, op=ALU.add)

            def divide_y(r, q):
                y = y_tiles[r][:, BANK * q : BANK * (q + 1)]
                engine = (LAST_DIVIDERS if r == TILES - 1 else DIVIDERS)[q]
                if engine == "scalar":
                    nc.scalar.activation(out=y, in_=y, func=ACT.Copy, scale=inverse[r][:])
                elif engine == "gpsimd":
                    nc.gpsimd.tensor_scalar(
                        out=y, in0=y, scalar1=inverse[r][:], scalar2=0.0, op0=ALU.mult, op1=ALU.add
                    )
                else:
                    nc.vector.tensor_scalar(out=y, in0=y, scalar1=inverse[r][:], scalar2=None, op0=ALU.mult)

            def store_y(r, half):
                cols = slice(2 * BANK * half, 2 * BANK * (half + 1))
                nc.sync.dma_start(out=out_0[P * r : P * (r + 1), cols], in_=y_tiles[r][:, cols])

            def run(step, r, *which):
                if 0 <= r < TILES:
                    step(r, *which)

            for n in range(-3, TILES + 1):
                run(stage2_z, n)
                run(add_y, n - 1, 2)
                run(stage2_r, n, 0)
                run(quantize_h, n + 2)
                run(divide_y, n - 1, 0)
                run(stage2_r, n, 1)
                run(divide_y, n - 1, 1)
                run(store_y, n - 1, 0)
                run(add_y, n - 1, 3)
                for half in range(2):
                    run(transpose_h, n + 3, half)
                    run(cap, n + 1, half)
                run(divide_y, n - 1, 2)
                run(stage2_r, n, 2)
                run(scale_e, n + 1)
                run(add_y, n, 0)
                run(divide_y, n - 1, 3)
                run(store_y, n - 1, 1)
                run(quantize_e, n + 1)
                run(square_z, n)
                run(stage1, n + 2, 0)
                run(invert_sigma, n)
                run(stage2_r, n, 3)
                run(stage1, n + 2, 1)
                run(square_y, n + 1)
                run(divide_z, n)
                run(store_z, n)
                run(copy_h, n + 3, 0)
                run(add_y, n, 1)
                run(copy_h, n + 3, 1)
                run(make_y, n + 2)
